import numpy as np
import ml_dtypes


def mxq(x, axis, fmt="e4m3"):
    dtype, down = {"e4m3": (ml_dtypes.float8_e4m3fn, 7), "e5m2": (ml_dtypes.float8_e5m2, 14)}[fmt]
    v = np.moveaxis(np.asarray(x, np.float32).astype(ml_dtypes.bfloat16).astype(np.float64), axis, -1)
    blocks = v.reshape(v.shape[:-1] + (-1, 32))
    amax = np.abs(blocks).max(-1, keepdims=True)
    byte = np.maximum(np.where(amax > 0, np.frexp(amax)[1] - 1 + 127, 0) - down, 1)
    scale = np.exp2(byte - 127.0)
    codes = (blocks / scale).astype(np.float32).astype(dtype).astype(np.float64)
    return np.moveaxis((codes * scale).reshape(v.shape), -1, axis)


WIDE = False


def mx_kscale(k):
    if not WIDE:
        return np.ones(k)
    levels = np.array([10, -10, 5, -5, 0])
    if k % 512:
        return np.exp2(np.random.permutation(np.resize(levels, k // 32))).repeat(32)
    a = np.empty((k // 512, 16))
    for p in range(k // 512):
        a[p, :8] = np.random.permutation(np.resize(levels, 8))
        for g in range(8):
            far = levels[np.abs(levels - a[p, g]) >= 10]
            a[p, g + 8] = far[np.random.randint(len(far))]
    return np.exp2(a.ravel()).repeat(32)


def f64(x):
    return np.asarray(x).astype(np.float64)


def striped(idx):
    return np.tile(idx.reshape(-1, 16).T, (8, 1)).astype(np.uint16)


def unstriped(offs):
    return offs[:16].T.reshape(-1).astype(np.int64)


E2M1 = np.array([0.0, 0.5, 1.0, 1.5, 2.0, 3.0, 4.0, 6.0, -0.0, -0.5, -1.0, -1.5, -2.0, -3.0, -4.0, -6.0])


def pack_weight(w, fmt):
    k, n = w.shape
    w = f64(np.asarray(w, np.float32).astype(ml_dtypes.bfloat16)).reshape(k // 32, 32, n)
    amax = np.abs(w).max(1)
    if fmt == "e4m3":
        byte = np.frexp(amax)[1] - 1 + 127 - 7
    else:
        mant, ex = np.frexp(amax / 6.0)
        byte = np.where(mant > 0.5, ex, ex - 1) + 127
    byte = np.clip(np.where(amax > 0, byte, 1), 1, 254)
    scaled = (w * np.exp2(127.0 - byte)[:, None, :]).reshape(k, n).astype(np.float32)
    by_word = np.ascontiguousarray(scaled.reshape(k // 512, 128, 4, n).transpose(0, 1, 3, 2))
    if fmt == "e4m3":
        words = by_word.astype(ml_dtypes.float8_e4m3fn).view(np.uint8)
    else:
        c = by_word.astype(ml_dtypes.float4_e2m1fn).view(np.uint8) & 0xF
        words = (c[..., 0::2] | (c[..., 1::2] << 4)).reshape(k // 512, 128, 2 * n)
    return np.ascontiguousarray(words), np.ascontiguousarray(byte.astype(np.uint8).reshape(k // 512, 16, n))


def unpack_weight(words, scales, fmt):
    g, _, n = scales.shape
    words = np.ascontiguousarray(words).reshape(g, 128, n, -1)
    if fmt == "e4m3":
        vals = words.view(ml_dtypes.float8_e4m3fn).astype(np.float64)
    else:
        nib = np.empty((g, 128, n, 4), np.uint8)
        nib[..., 0::2] = words & 0xF
        nib[..., 1::2] = words >> 4
        vals = E2M1[nib]
    vals = vals * np.repeat(np.exp2(scales.astype(np.float64) - 127.0), 8, axis=1)[..., None]
    return vals.transpose(0, 1, 3, 2).reshape(g * 512, n)


def silu(v):
    return v / (1.0 + np.exp(-np.maximum(v, -700.0)))


K, T, E, C, H, N = 512, 1024, 4, 256, 512, 256


def by_expert(wq, xq):
    return np.concatenate([wq[e].T @ xq[:, e * C:(e + 1) * C] for e in range(E)], axis=1)


def setup_inputs():
    n = np.random.standard_normal
    s = mx_kscale(K)[:, None]
    u = mx_kscale(H)
    w1 = [pack_weight(m, "e2m1") for m in n((E, K, H)) / np.sqrt(K) / s[None]]
    w3 = [pack_weight(m, "e2m1") for m in n((E, K, H)) / np.sqrt(K) / s[None] * u[None, None, :]]
    w2 = [pack_weight(m, "e2m1") for m in n((E, H, N)) / np.sqrt(H) / u[None, :, None]]
    return {
        "xT": (n((K, T)) * s).astype(np.float32),
        "w1_words": np.stack([m[0] for m in w1]),
        "w1_scales": np.stack([m[1] for m in w1]),
        "w3_words": np.stack([m[0] for m in w3]),
        "w3_scales": np.stack([m[1] for m in w3]),
        "w2_words": np.stack([m[0] for m in w2]),
        "w2_scales": np.stack([m[1] for m in w2]),
        "gate": np.tile(np.random.uniform(0.2, 1.0, E * C), (N, 1)).astype(np.float32),
        "offs": striped(np.random.permutation(T)[:E * C]),
        "dst": striped(np.random.permutation(T)[:E * C]),
    }


def reference(xT, w1_words, w1_scales, w3_words, w3_scales, w2_words, w2_scales, gate, offs, dst):
    idx = unstriped(offs)
    w1 = np.stack([unpack_weight(w1_words[e], w1_scales[e], "e2m1") for e in range(E)])
    w3 = np.stack([unpack_weight(w3_words[e], w3_scales[e], "e2m1") for e in range(E)])
    w2 = np.stack([unpack_weight(w2_words[e], w2_scales[e], "e2m1") for e in range(E)])
    xq = mxq(f64(xT)[:, idx], 0, "e4m3")
    h = silu(by_expert(w1, xq))
    h = h * by_expert(w3, xq)
    y = by_expert(w2, mxq(h, 0, "e4m3"))
    out = np.zeros((N, T))
    out[:, unstriped(dst)] = f64(gate) * y
    return out

@@ -1,0 +1,189 @@
+from contextlib import ExitStack
+
+import concourse.mybir as mybir
+from concourse.masks import make_identity
+
+K, T, E, C, H, N = 512, 1024, 4, 256, 512, 256
+FLOPS = 2 * E * C * (K * H + K * H + H * N)
+
+P = 128
+BLK = 128
+NBLK = E * C // BLK
+CHUNKS = (512, 256, 256)
+
+F32 = mybir.dt.float32
+BF16 = mybir.dt.bfloat16
+I32 = mybir.dt.int32
+U32 = mybir.dt.uint32
+U16 = mybir.dt.uint16
+U8 = mybir.dt.uint8
+FP8 = mybir.dt.float8_e4m3fn_x4
+FP4 = mybir.dt.float4_e2m1fn_x4
+ACT = mybir.ActivationFunctionType
+MULT = mybir.AluOpType.mult
+
+
+def tile_moe_two_glu_silu_kernel(
+    tc, xT, w1_words, w1_scales, w3_words, w3_scales, w2_words, w2_scales, gate, offs, dst, out
+):
+    nc = tc.nc
+    with ExitStack() as ctx:
+        keep = ctx.enter_context(tc.tile_pool(name="keep", bufs=1))
+        work = ctx.enter_context(tc.tile_pool(name="work", bufs=8))
+        psum = ctx.enter_context(tc.psum_pool(name="psum", bufs=1))
+
+        offs_sb = keep.tile([P, E * C // 16], U16, name="offs_sb")
+        dst_sb = keep.tile([P, E * C // 16], U16, name="dst_sb")
+        w1s = keep.tile([P, E * H], U8, name="w1s", align_bytes=256)
+        w3a = keep.tile([P, H], U8, name="w3a", align_bytes=256)
+        w3b = keep.tile([P, (E - 1) * H], U8, name="w3b", align_bytes=256)
+        w2s = keep.tile([P, E * N], U8, name="w2s", align_bytes=256)
+        xsc = keep.tile([P, T], U8, name="xsc", align_bytes=256)
+        xcd = keep.tile([P, T], U32, name="xcd", align_bytes=256)
+        ident = keep.tile([P, P], F32, name="ident", align_bytes=256)
+        gate_sb = keep.tile([P, 2, E * C], F32, name="gate_sb", align_bytes=256)
+        win = [keep.tile([P, T], F32, name=f"win{m}", align_bytes=256) for m in range(2)]
+
+        for plane in (w3a, w1s, w3b, w2s):
+            nc.vector.memset(plane[:].bitcast(I32), 0)
+        warm = keep.tile([P, 1], F32, name="warm")
+        nc.vector.memset(warm[:], 0.0)
+        nc.gpsimd.memset(xsc[:].bitcast(I32), 0)
+
+        def load_scales(eng, plane, src, e0=0, n=E):
+            for q in range(4):
+                eng.dma_start(
+                    out=plane[32 * q : 32 * q + 4, :].rearrange("r (e i) -> r e i", e=n).bitcast(I32),
+                    in_=src[e0 : e0 + n, 0, 4 * q : 4 * q + 4, :].rearrange("e r i -> r e i").bitcast(I32),
+                )
+
+        xin = xT.rearrange("(p j) t -> p j t", j=4)
+        xf = []
+        c0 = 0
+        for i, w in enumerate(CHUNKS):
+            t = keep.tile([P, 4, w], F32, name=f"xf{i}", align_bytes=256)
+            nc.sync.dma_start(out=t[:], in_=xin[:, :, c0 : c0 + w])
+            xf.append(t)
+            c0 += w
+        nc.sync.dma_start(offs_sb[:], offs)
+        load_scales(nc.sync, w1s, w1_scales)
+        load_scales(nc.gpsimd, w3a, w3_scales, 0, 1)
+        nc.scalar.activation(warm[:], warm[:], ACT.Silu)
+        make_identity(nc, ident[:])
+        load_scales(nc.gpsimd, w3b, w3_scales, 1, 3)
+
+        wt = {}
+
+        def load_w(key, src, e0, n):
+            width = src.shape[3]
+            t = keep.tile([P, n, width], U8, name=f"{key}_{e0}", align_bytes=256)
+            nc.sync.dma_start(out=t[:].bitcast(I32), in_=src[e0 : e0 + n, 0].rearrange("e p b -> p e b").bitcast(I32))
+            for i in range(n):
+                wt[key, e0 + i] = t[:, i, :]
+
+        load_w("w1", w1_words, 0, 1)
+        load_w("w3", w3_words, 0, 1)
+        load_w("w1", w1_words, 1, 3)
+        load_w("w3", w3_words, 1, 3)
+        load_scales(nc.sync, w2s, w2_scales)
+        load_w("w2", w2_words, 0, 4)
+        nc.sync.dma_start(dst_sb[:], dst)
+        nc.sync.dma_start(out=gate_sb[:], in_=gate.rearrange("(m p) j -> p m j", m=2))
+
+        for i, lo, w, caster in ((0, 0, 256, "s"), (0, 256, 256, "v"), (1, 0, 256, "v"), (2, 0, 128, "s"), (2, 128, 128, "v")):
+            xb = keep.tile([P, w, 4], BF16, name=f"xb{i}_{lo}", align_bytes=256)
+            src = xf[i][:, :, lo : lo + w].rearrange("p j w -> p w j")
+            if caster == "s":
+                nc.scalar.copy(xb[:], src)
+            else:
+                nc.vector.tensor_copy(xb[:], src)
+            c0 = sum(CHUNKS[:i]) + lo
+            nc.vector.quantize_mx(
+                out=xcd[:, c0 : c0 + w].bitcast(FP8), scales=xsc[:, c0 : c0 + w], in_=xb[:].rearrange("p w j -> p (w j)")
+            )
+
+        codes, scales = {}, {}
+
+        def gather(b, n):
+            cols = slice(b * BLK // 16, (b + n) * BLK // 16)
+            cd = keep.tile([P, n * BLK], U32, name=f"cd{b}", align_bytes=256)
+            sc = keep.tile([P, n * BLK], U8, name=f"sc{b}", align_bytes=256)
+            nc.vector.tensor_copy(cd[:], xcd[:].indirect(offs_sb[:, cols]))
+            nc.vector.tensor_copy(sc[:], xsc[:].indirect(offs_sb[:, cols]))
+            for i in range(n):
+                codes[b + i], scales[b + i] = cd[:, i * BLK : (i + 1) * BLK], sc[:, i * BLK : (i + 1) * BLK]
+
+        st = {}
+
+        def project(b):
+            e = b // 2
+            pa = psum.tile([P, H], F32, name="pa", bufs=2)
+            pb = psum.tile([P, H], F32, name="pb", bufs=3)
+            w3s = w3a[:] if e == 0 else w3b[:, (e - 1) * H : e * H]
+            for ps, key, plane in ((pa, "w1", w1s[:, e * H : (e + 1) * H]), (pb, "w3", w3s)):
+                nc.tensor.matmul_mx(
+                    out=ps[:],
+                    lhsT=codes[b].bitcast(FP8),
+                    lhsT_scale=scales[b],
+                    rhs=wt[key, e].bitcast(FP4),
+                    rhs_scale=plane,
+                    start=True,
+                    stop=True,
+                )
+            sil = work.tile([P, H], F32, name="sil", align_bytes=256)
+            nc.scalar.activation(sil[:], pa[:], ACT.Silu)
+            st["sil", b], st["pb", b] = sil, pb
+
+        def product(b):
+            h = work.tile([P, H], BF16, name="h", align_bytes=256)
+            nc.vector.tensor_tensor(h[:], st["sil", b][:], st["pb", b][:], MULT)
+            words = h[:].bitcast(F32)
+            pt = psum.tile([P, 2, BLK], F32, name="pt")
+            for u in range(2):
+                nc.tensor.transpose(pt[:, u, :], words[:, u : H // 2 : 2], ident[:])
+            hg = work.tile([P, BLK, 4], BF16, name="hg", align_bytes=256)
+            nc.scalar.copy(hg[:].rearrange("p s t -> p (s t)").bitcast(F32).rearrange("p (s u) -> p s u", u=2), pt[:].rearrange("p u s -> p s u"))
+            st["hg", b] = hg
+
+        def down(b):
+            e = b // 2
+            hc = work.tile([P, BLK], U32, name="hc", align_bytes=256)
+            hs = work.tile([P, BLK], U8, name="hs", align_bytes=256)
+            nc.vector.quantize_mx(out=hc[:].bitcast(FP8), scales=hs[:], in_=st["hg", b][:].rearrange("p s t -> p (s t)"))
+            py = psum.tile([P, 2, BLK], F32, name="py", bufs=2)
+            for m in range(2):
+                nc.tensor.matmul_mx(
+                    out=py[:, m, :],
+                    lhsT=wt["w2", e][:, m * 256 : m * 256 + 256].bitcast(FP4),
+                    lhsT_scale=w2s[:, e * N + m * P : e * N + m * P + P],
+                    rhs=hc[:].bitcast(FP8),
+                    rhs_scale=hs[:],
+                    start=True,
+                    stop=True,
+                )
+            ys = work.tile([P, 2, BLK], F32, name="ys", align_bytes=256)
+            nc.scalar.copy(ys[:], py[:])
+            st["ys", b] = ys
+
+        def place(b, m):
+            cols = slice(b * BLK // 16, (b + 1) * BLK // 16)
+            nc.vector.tensor_tensor(win[m][:].indirect(dst_sb[:, cols]), st["ys", b][:, m, :], gate_sb[:, m, b * BLK : (b + 1) * BLK], MULT)
+
+        gathers = {0: ((0, 1), (1, 1)), 1: ((2, 2),), 3: ((4, 2),), 4: ((6, 2),)}
+        for s in range(NBLK + 3):
+            for g in gathers.get(s, ()):
+                gather(*g)
+            if s < NBLK:
+                project(s)
+            if 1 <= s <= NBLK:
+                product(s - 1)
+            if 2 <= s <= NBLK + 1:
+                down(s - 2)
+            if 3 <= s < NBLK + 1:
+                place(s - 3, 0)
+                place(s - 3, 1)
+        for m in range(2):
+            for b in (NBLK - 2, NBLK - 1):
+                place(b, m)
+        for m in range(2):
+            nc.sync.dma_start(out=out[m * P : (m + 1) * P, :], in_=win[m][:])

@@ -9,7 +9,7 @@ FLOPS = 2 * E * C * (K * H + K * H + H * N)
 P = 128
 BLK = 128
 NBLK = E * C // BLK
-CHUNKS = (512, 256, 256)
+GROUPS = ((0, 1), (1, 1), (2, 2), (4, 2), (6, 2))
 
 F32 = mybir.dt.float32
 BF16 = mybir.dt.bfloat16
@@ -35,42 +35,40 @@ def tile_moe_two_glu_silu_kernel(
         offs_sb = keep.tile([P, E * C // 16], U16, name="offs_sb")
         dst_sb = keep.tile([P, E * C // 16], U16, name="dst_sb")
         w1s = keep.tile([P, E * H], U8, name="w1s", align_bytes=256)
-        w3a = keep.tile([P, H], U8, name="w3a", align_bytes=256)
-        w3b = keep.tile([P, (E - 1) * H], U8, name="w3b", align_bytes=256)
+        w3s = keep.tile([P, E * H], U8, name="w3s", align_bytes=256)
         w2s = keep.tile([P, E * N], U8, name="w2s", align_bytes=256)
-        xsc = keep.tile([P, T], U8, name="xsc", align_bytes=256)
-        xcd = keep.tile([P, T], U32, name="xcd", align_bytes=256)
+        pairs = [keep.tile([P, T], U32, name=f"pairs{u}", align_bytes=256) for u in range(2)]
         ident = keep.tile([P, P], F32, name="ident", align_bytes=256)
-        gate_sb = keep.tile([P, 2, E * C], F32, name="gate_sb", align_bytes=256)
+        gate_sb = keep.tile([P, E * C], F32, name="gate_sb", align_bytes=256)
+        stage = keep.tile([P, 6 * 256], U32, name="stage", align_bytes=256)
         win = [keep.tile([P, T], F32, name=f"win{m}", align_bytes=256) for m in range(2)]
 
-        for plane in (w3a, w1s, w3b, w2s):
+        for plane in (w1s, w3s, w2s):
             nc.vector.memset(plane[:].bitcast(I32), 0)
         warm = keep.tile([P, 1], F32, name="warm")
         nc.vector.memset(warm[:], 0.0)
-        nc.gpsimd.memset(xsc[:].bitcast(I32), 0)
 
-        def load_scales(eng, plane, src, e0=0, n=E):
+        def load_scales(eng, plane, src):
             for q in range(4):
                 eng.dma_start(
-                    out=plane[32 * q : 32 * q + 4, :].rearrange("r (e i) -> r e i", e=n).bitcast(I32),
-                    in_=src[e0 : e0 + n, 0, 4 * q : 4 * q + 4, :].rearrange("e r i -> r e i").bitcast(I32),
+                    out=plane[32 * q : 32 * q + 4, :].rearrange("r (e i) -> r e i", e=E).bitcast(I32),
+                    in_=src[:, 0, 4 * q : 4 * q + 4, :].rearrange("e r i -> r e i").bitcast(I32),
                 )
 
         xin = xT.rearrange("(p j) t -> p j t", j=4)
+        CH = ((0, 0, 512, 512), (0, 512, 512, 384), (1, 0, 384, 0), (1, 384, 384, 0), (1, 768, 256, 256))
         xf = []
-        c0 = 0
-        for i, w in enumerate(CHUNKS):
-            t = keep.tile([P, 4, w], F32, name=f"xf{i}", align_bytes=256)
-            nc.sync.dma_start(out=t[:], in_=xin[:, :, c0 : c0 + w])
+        for i, (u, c0, w, nv) in enumerate(CH):
+            if i == len(CH) - 1:
+                t = stage[:, 0:512].bitcast(F32).rearrange("p (u s) -> p u s", u=2)
+            else:
+                t = keep.tile([P, 2, w], F32, name=f"xf{i}", align_bytes=256)[:]
+            nc.sync.dma_start(out=t, in_=xin[:, 2 * u : 2 * u + 2, c0 : c0 + w])
             xf.append(t)
-            c0 += w
-        nc.sync.dma_start(offs_sb[:], offs)
-        load_scales(nc.sync, w1s, w1_scales)
-        load_scales(nc.gpsimd, w3a, w3_scales, 0, 1)
+            if i == 0:
+                nc.sync.dma_start(offs_sb[:], offs)
         nc.scalar.activation(warm[:], warm[:], ACT.Silu)
         make_identity(nc, ident[:])
-        load_scales(nc.gpsimd, w3b, w3_scales, 1, 3)
 
         wt = {}
 
@@ -82,36 +80,49 @@ def tile_moe_two_glu_silu_kernel(
                 wt[key, e0 + i] = t[:, i, :]
 
         load_w("w1", w1_words, 0, 1)
+        load_scales(nc.sync, w1s, w1_scales)
         load_w("w3", w3_words, 0, 1)
+        load_scales(nc.scalar, w3s, w3_scales)
         load_w("w1", w1_words, 1, 3)
         load_w("w3", w3_words, 1, 3)
-        load_scales(nc.sync, w2s, w2_scales)
         load_w("w2", w2_words, 0, 4)
         nc.sync.dma_start(dst_sb[:], dst)
-        nc.sync.dma_start(out=gate_sb[:], in_=gate.rearrange("(m p) j -> p m j", m=2))
+        load_scales(nc.gpsimd, w2s, w2_scales)
+        nc.sync.dma_start(out=gate_sb[:], in_=gate[0:P, :])
 
-        for i, lo, w, caster in ((0, 0, 256, "s"), (0, 256, 256, "v"), (1, 0, 256, "v"), (2, 0, 128, "s"), (2, 128, 128, "v")):
-            xb = keep.tile([P, w, 4], BF16, name=f"xb{i}_{lo}", align_bytes=256)
-            src = xf[i][:, :, lo : lo + w].rearrange("p j w -> p w j")
-            if caster == "s":
-                nc.scalar.copy(xb[:], src)
-            else:
-                nc.vector.tensor_copy(xb[:], src)
-            c0 = sum(CHUNKS[:i]) + lo
-            nc.vector.quantize_mx(
-                out=xcd[:, c0 : c0 + w].bitcast(FP8), scales=xsc[:, c0 : c0 + w], in_=xb[:].rearrange("p w j -> p (w j)")
-            )
+        def cast(i):
+            u, c0, w, nv = CH[i]
+            for lo, hi, copy in ((0, nv, nc.vector.tensor_copy), (nv, w, nc.scalar.copy)):
+                if hi > lo:
+                    dstv = pairs[u][:, c0 + lo : c0 + hi].bitcast(BF16).rearrange("p (w j) -> p w j", j=2)
+                    copy(dstv, xf[i][:, :, lo:hi].rearrange("p j w -> p w j"))
+
+        start = {0: 3, 1: 5, 2: 2, 3: 4, 4: 1}
+        picked = {g: stage[:, 256 * start[g] : 256 * start[g] + 2 * n * BLK].rearrange("p (u s) -> p u s", u=2) for g, (b, n) in enumerate(GROUPS)}
+
+        def gather(g, u):
+            b, n = GROUPS[g]
+            cols = slice(b * BLK // 16, (b + n) * BLK // 16)
+            nc.vector.tensor_copy(picked[g][:, u, :], pairs[u][:].indirect(offs_sb[:, cols]))
 
         codes, scales = {}, {}
 
-        def gather(b, n):
-            cols = slice(b * BLK // 16, (b + n) * BLK // 16)
+        def quantise(g):
+            b, n = GROUPS[g]
+            xg = keep.tile([P, n * BLK, 2], U32, name=f"xg{g}", align_bytes=256)
+            nc.scalar.copy(xg[:], picked[g].rearrange("p u s -> p s u"))
             cd = keep.tile([P, n * BLK], U32, name=f"cd{b}", align_bytes=256)
             sc = keep.tile([P, n * BLK], U8, name=f"sc{b}", align_bytes=256)
-            nc.vector.tensor_copy(cd[:], xcd[:].indirect(offs_sb[:, cols]))
-            nc.vector.tensor_copy(sc[:], xsc[:].indirect(offs_sb[:, cols]))
+            nc.vector.quantize_mx(out=cd[:].bitcast(FP8), scales=sc[:], in_=xg[:].rearrange("p s u -> p (s u)").bitcast(BF16))
             for i in range(n):
                 codes[b + i], scales[b + i] = cd[:, i * BLK : (i + 1) * BLK], sc[:, i * BLK : (i + 1) * BLK]
+
+        cast(0)
+        cast(1)
+        for g in range(4):
+            gather(g, 0)
+        for i in (2, 3, 4):
+            cast(i)
 
         st = {}
 
@@ -119,14 +130,13 @@ def tile_moe_two_glu_silu_kernel(
             e = b // 2
             pa = psum.tile([P, H], F32, name="pa", bufs=2)
             pb = psum.tile([P, H], F32, name="pb", bufs=3)
-            w3s = w3a[:] if e == 0 else w3b[:, (e - 1) * H : e * H]
-            for ps, key, plane in ((pa, "w1", w1s[:, e * H : (e + 1) * H]), (pb, "w3", w3s)):
+            for ps, key, plane in ((pa, "w1", w1s), (pb, "w3", w3s)):
                 nc.tensor.matmul_mx(
                     out=ps[:],
                     lhsT=codes[b].bitcast(FP8),
                     lhsT_scale=scales[b],
                     rhs=wt[key, e].bitcast(FP4),
-                    rhs_scale=plane,
+                    rhs_scale=plane[:, e * H : (e + 1) * H],
                     start=True,
                     stop=True,
                 )
@@ -167,23 +177,26 @@ def tile_moe_two_glu_silu_kernel(
 
         def place(b, m):
             cols = slice(b * BLK // 16, (b + 1) * BLK // 16)
-            nc.vector.tensor_tensor(win[m][:].indirect(dst_sb[:, cols]), st["ys", b][:, m, :], gate_sb[:, m, b * BLK : (b + 1) * BLK], MULT)
+            nc.vector.tensor_tensor(win[m][:].indirect(dst_sb[:, cols]), st["ys", b][:, m, :], gate_sb[:, b * BLK : (b + 1) * BLK], MULT)
 
-        gathers = {0: ((0, 1), (1, 1)), 1: ((2, 2),), 3: ((4, 2),), 4: ((6, 2),)}
+        first = {b: g for g, (b, n) in enumerate(GROUPS)}
+        gather(0, 1)
+        gather(1, 1)
+        gather(4, 0)
         for s in range(NBLK + 3):
-            for g in gathers.get(s, ()):
-                gather(*g)
+            if s in first:
+                g = first[s]
+                quantise(g)
+                if g + 2 < len(GROUPS):
+                    gather(g + 2, 1)
             if s < NBLK:
                 project(s)
             if 1 <= s <= NBLK:
                 product(s - 1)
             if 2 <= s <= NBLK + 1:
                 down(s - 2)
-            if 3 <= s < NBLK + 1:
+            if 3 <= s < NBLK + 3:
                 place(s - 3, 0)
                 place(s - 3, 1)
-        for m in range(2):
-            for b in (NBLK - 2, NBLK - 1):
-                place(b, m)
         for m in range(2):
             nc.sync.dma_start(out=out[m * P : (m + 1) * P, :], in_=win[m][:])

@@ -35,15 +35,14 @@ def tile_moe_two_glu_silu_kernel(
         offs_sb = keep.tile([P, E * C // 16], U16, name="offs_sb")
         dst_sb = keep.tile([P, E * C // 16], U16, name="dst_sb")
         w1s = keep.tile([P, E * H], U8, name="w1s", align_bytes=256)
-        w3s = keep.tile([P, E * H], U8, name="w3s", align_bytes=256)
         w2s = keep.tile([P, E * N], U8, name="w2s", align_bytes=256)
         pairs = [keep.tile([P, T], U32, name=f"pairs{u}", align_bytes=256) for u in range(2)]
         ident = keep.tile([P, P], F32, name="ident", align_bytes=256)
         gate_sb = keep.tile([P, E * C], F32, name="gate_sb", align_bytes=256)
-        stage = keep.tile([P, 6 * 256], U32, name="stage", align_bytes=256)
+        stage = keep.tile([P, 7 * 256], U32, name="stage", align_bytes=256)
         win = [keep.tile([P, T], F32, name=f"win{m}", align_bytes=256) for m in range(2)]
 
-        for plane in (w1s, w3s, w2s):
+        for plane in (w1s, w2s):
             nc.vector.memset(plane[:].bitcast(I32), 0)
         warm = keep.tile([P, 1], F32, name="warm")
         nc.vector.memset(warm[:], 0.0)
@@ -59,10 +58,10 @@ def tile_moe_two_glu_silu_kernel(
         CH = ((0, 0, 512, 512), (0, 512, 512, 384), (1, 0, 384, 0), (1, 384, 384, 0), (1, 768, 256, 256))
         xf = []
         for i, (u, c0, w, nv) in enumerate(CH):
-            if i == len(CH) - 1:
-                t = stage[:, 0:512].bitcast(F32).rearrange("p (u s) -> p u s", u=2)
+            if i == 3:
+                t = stage[:, 0:768].bitcast(F32).rearrange("p (u s) -> p u s", u=2)
             else:
-                t = keep.tile([P, 2, w], F32, name=f"xf{i}", align_bytes=256)[:]
+                t = keep.tile([P, 2, w], F32, name=f"xf{i}", align_bytes=256, tag=f"xf{i}")[:]
             nc.sync.dma_start(out=t, in_=xin[:, 2 * u : 2 * u + 2, c0 : c0 + w])
             xf.append(t)
             if i == 0:
@@ -82,12 +81,11 @@ def tile_moe_two_glu_silu_kernel(
         load_w("w1", w1_words, 0, 1)
         load_scales(nc.sync, w1s, w1_scales)
         load_w("w3", w3_words, 0, 1)
-        load_scales(nc.scalar, w3s, w3_scales)
         load_w("w1", w1_words, 1, 3)
         load_w("w3", w3_words, 1, 3)
         load_w("w2", w2_words, 0, 4)
+        load_scales(nc.sync, w2s, w2_scales)
         nc.sync.dma_start(dst_sb[:], dst)
-        load_scales(nc.gpsimd, w2s, w2_scales)
         nc.sync.dma_start(out=gate_sb[:], in_=gate[0:P, :])
 
         def cast(i):
@@ -97,13 +95,14 @@ def tile_moe_two_glu_silu_kernel(
                     dstv = pairs[u][:, c0 + lo : c0 + hi].bitcast(BF16).rearrange("p (w j) -> p w j", j=2)
                     copy(dstv, xf[i][:, :, lo:hi].rearrange("p j w -> p w j"))
 
-        start = {0: 3, 1: 5, 2: 2, 3: 4, 4: 1}
+        start = {0: 4, 1: 6, 2: 3, 3: 5, 4: 2}
         picked = {g: stage[:, 256 * start[g] : 256 * start[g] + 2 * n * BLK].rearrange("p (u s) -> p u s", u=2) for g, (b, n) in enumerate(GROUPS)}
 
-        def gather(g, u):
+        def gather(g, u, lo=0, hi=None):
             b, n = GROUPS[g]
-            cols = slice(b * BLK // 16, (b + n) * BLK // 16)
-            nc.vector.tensor_copy(picked[g][:, u, :], pairs[u][:].indirect(offs_sb[:, cols]))
+            hi = n if hi is None else hi
+            cols = slice((b + lo) * BLK // 16, (b + hi) * BLK // 16)
+            nc.vector.tensor_copy(picked[g][:, u, lo * BLK : hi * BLK], pairs[u][:].indirect(offs_sb[:, cols]))
 
         codes, scales = {}, {}
 
@@ -118,11 +117,20 @@ def tile_moe_two_glu_silu_kernel(
                 codes[b + i], scales[b + i] = cd[:, i * BLK : (i + 1) * BLK], sc[:, i * BLK : (i + 1) * BLK]
 
         cast(0)
+        jc = keep.tile([P, BLK], U32, name="jc", align_bytes=256)
+        js = keep.tile([P, BLK], U8, name="js", align_bytes=256)
+        nc.vector.quantize_mx(out=jc[:].bitcast(FP8), scales=js[:], in_=pairs[0][:, 0:256].bitcast(BF16))
+        pw = psum.tile([P, H], F32, name="pt")
+        for i in range(4):
+            nc.tensor.matmul_mx(out=pw[:], lhsT=jc[:].bitcast(FP8), lhsT_scale=js[:], rhs=wt["w1", 0].bitcast(FP4), rhs_scale=w1s[:, 0:H], start=True, stop=True)
         cast(1)
+        w3s = keep.tile([P, E * H], U8, name="w3s", align_bytes=256, tag="xf1")
+        nc.vector.memset(w3s[:].bitcast(I32), 0)
         for g in range(4):
             gather(g, 0)
         for i in (2, 3, 4):
             cast(i)
+        load_scales(nc.scalar, w3s, w3_scales)
 
         st = {}
 
@@ -182,7 +190,8 @@ def tile_moe_two_glu_silu_kernel(
         first = {b: g for g, (b, n) in enumerate(GROUPS)}
         gather(0, 1)
         gather(1, 1)
-        gather(4, 0)
+        gather(4, 0, 0, 1)
+        gather(4, 0, 1, 2)
         for s in range(NBLK + 3):
             if s in first:
                 g = first[s]

@@ -116,13 +116,15 @@ def tile_moe_two_glu_silu_kernel(
             for i in range(n):
                 codes[b + i], scales[b + i] = cd[:, i * BLK : (i + 1) * BLK], sc[:, i * BLK : (i + 1) * BLK]
 
-        cast(0)
-        jc = keep.tile([P, BLK], U32, name="jc", align_bytes=256)
-        js = keep.tile([P, BLK], U8, name="js", align_bytes=256)
-        nc.vector.quantize_mx(out=jc[:].bitcast(FP8), scales=js[:], in_=pairs[0][:, 0:256].bitcast(BF16))
+        jz = keep.tile([P, 4 * H], BF16, name="jz", align_bytes=256)
+        jc = keep.tile([P, H], U32, name="jc", align_bytes=256)
+        js = keep.tile([P, H], U8, name="js", align_bytes=256)
+        nc.vector.memset(jz[:].bitcast(I32), 0)
+        nc.vector.quantize_mx(out=jc[:].bitcast(FP8), scales=js[:], in_=jz[:])
         pw = psum.tile([P, H], F32, name="pt")
         for i in range(4):
-            nc.tensor.matmul_mx(out=pw[:], lhsT=jc[:].bitcast(FP8), lhsT_scale=js[:], rhs=wt["w1", 0].bitcast(FP4), rhs_scale=w1s[:, 0:H], start=True, stop=True)
+            nc.tensor.matmul_mx(out=pw[:], lhsT=wt["w1", 0][:, 0:256].bitcast(FP4), lhsT_scale=js[:, 0:P], rhs=jc[:].bitcast(FP8), rhs_scale=js[:], start=True, stop=True)
+        cast(0)
         cast(1)
         w3s = keep.tile([P, E * H], U8, name="w3s", align_bytes=256, tag="xf1")
         nc.vector.memset(w3s[:].bitcast(I32), 0)

@@ -9,7 +9,19 @@ FLOPS = 2 * E * C * (K * H + K * H + H * N)
 P = 128
 BLK = 128
 NBLK = E * C // BLK
+LIST = 16
+
 GROUPS = ((0, 1), (1, 1), (2, 2), (4, 2), (6, 2))
+LAST_GROUP = len(GROUPS) - 1
+
+CHUNKS = ((0, 0, 704, 704), (0, 704, 320, 224), (1, 0, 448, 0), (1, 448, 384, 0), (1, 832, 192, 192))
+STAGED_CHUNK = 3
+W3_PLANE_CHUNK = 1
+
+REGION = 256
+FIRST_REGION = (4, 6, 3, 5, 2)
+
+WARM_PASSES = 4
 
 F32 = mybir.dt.float32
 BF16 = mybir.dt.bfloat16
@@ -29,23 +41,23 @@ def tile_moe_two_glu_silu_kernel(
     nc = tc.nc
     with ExitStack() as ctx:
         keep = ctx.enter_context(tc.tile_pool(name="keep", bufs=1))
-        work = ctx.enter_context(tc.tile_pool(name="work", bufs=8))
+        work = ctx.enter_context(tc.tile_pool(name="work", bufs=NBLK))
         psum = ctx.enter_context(tc.psum_pool(name="psum", bufs=1))
 
-        offs_sb = keep.tile([P, E * C // 16], U16, name="offs_sb")
-        dst_sb = keep.tile([P, E * C // 16], U16, name="dst_sb")
+        offs_sb = keep.tile([P, E * C // LIST], U16, name="offs_sb")
+        dst_sb = keep.tile([P, E * C // LIST], U16, name="dst_sb")
         w1s = keep.tile([P, E * H], U8, name="w1s", align_bytes=256)
         w2s = keep.tile([P, E * N], U8, name="w2s", align_bytes=256)
         pairs = [keep.tile([P, T], U32, name=f"pairs{u}", align_bytes=256) for u in range(2)]
         ident = keep.tile([P, P], F32, name="ident", align_bytes=256)
         gate_sb = keep.tile([P, E * C], F32, name="gate_sb", align_bytes=256)
-        stage = keep.tile([P, 7 * 256], U32, name="stage", align_bytes=256)
+        stage = keep.tile([P, 7 * REGION], U32, name="stage", align_bytes=256)
         win = [keep.tile([P, T], F32, name=f"win{m}", align_bytes=256) for m in range(2)]
 
         for plane in (w1s, w2s):
             nc.vector.memset(plane[:].bitcast(I32), 0)
-        warm = keep.tile([P, 1], F32, name="warm")
-        nc.vector.memset(warm[:], 0.0)
+        table_warm = keep.tile([P, 1], F32, name="warm")
+        nc.vector.memset(table_warm[:], 0.0)
 
         def load_scales(eng, plane, src):
             for q in range(4):
@@ -54,128 +66,143 @@ def tile_moe_two_glu_silu_kernel(
                     in_=src[:, 0, 4 * q : 4 * q + 4, :].rearrange("e r i -> r e i").bitcast(I32),
                 )
 
-        xin = xT.rearrange("(p j) t -> p j t", j=4)
-        CH = ((0, 0, 512, 512), (0, 512, 512, 384), (1, 0, 384, 0), (1, 384, 384, 0), (1, 768, 256, 256))
-        xf = []
-        for i, (u, c0, w, nv) in enumerate(CH):
-            if i == 3:
-                t = stage[:, 0:768].bitcast(F32).rearrange("p (u s) -> p u s", u=2)
+        x_rows = xT.rearrange("(p j) t -> p j t", j=4)
+        raw = []
+        for i, (u, t0, width, by_vector) in enumerate(CHUNKS):
+            if i == STAGED_CHUNK:
+                chunk = stage[:, 0 : 2 * width].bitcast(F32).rearrange("p (j t) -> p j t", j=2)
             else:
-                t = keep.tile([P, 2, w], F32, name=f"xf{i}", align_bytes=256, tag=f"xf{i}")[:]
-            nc.sync.dma_start(out=t, in_=xin[:, 2 * u : 2 * u + 2, c0 : c0 + w])
-            xf.append(t)
+                chunk = keep.tile([P, 2, width], F32, name=f"xf{i}", align_bytes=256, tag=f"xf{i}")[:]
+            nc.sync.dma_start(out=chunk, in_=x_rows[:, 2 * u : 2 * u + 2, t0 : t0 + width])
+            raw.append(chunk)
             if i == 0:
                 nc.sync.dma_start(offs_sb[:], offs)
-        nc.scalar.activation(warm[:], warm[:], ACT.Silu)
+        nc.scalar.activation(table_warm[:], table_warm[:], ACT.Silu)
         make_identity(nc, ident[:])
 
-        wt = {}
+        weights = {}
 
-        def load_w(key, src, e0, n):
-            width = src.shape[3]
-            t = keep.tile([P, n, width], U8, name=f"{key}_{e0}", align_bytes=256)
-            nc.sync.dma_start(out=t[:].bitcast(I32), in_=src[e0 : e0 + n, 0].rearrange("e p b -> p e b").bitcast(I32))
+        def load_words(key, src, e0, n):
+            tile = keep.tile([P, n, src.shape[3]], U8, name=f"{key}_{e0}", align_bytes=256)
+            nc.sync.dma_start(out=tile[:].bitcast(I32), in_=src[e0 : e0 + n, 0].rearrange("e p b -> p e b").bitcast(I32))
             for i in range(n):
-                wt[key, e0 + i] = t[:, i, :]
+                weights[key, e0 + i] = tile[:, i, :]
 
-        load_w("w1", w1_words, 0, 1)
+        load_words("w1", w1_words, 0, 1)
         load_scales(nc.sync, w1s, w1_scales)
-        load_w("w3", w3_words, 0, 1)
-        load_w("w1", w1_words, 1, 3)
-        load_w("w3", w3_words, 1, 3)
-        load_w("w2", w2_words, 0, 4)
+        load_words("w3", w3_words, 0, 1)
+        load_words("w1", w1_words, 1, E - 1)
+        load_words("w3", w3_words, 1, E - 1)
+        load_words("w2", w2_words, 0, E)
         load_scales(nc.sync, w2s, w2_scales)
         nc.sync.dma_start(dst_sb[:], dst)
         nc.sync.dma_start(out=gate_sb[:], in_=gate[0:P, :])
 
         def cast(i):
-            u, c0, w, nv = CH[i]
-            for lo, hi, copy in ((0, nv, nc.vector.tensor_copy), (nv, w, nc.scalar.copy)):
+            u, t0, width, by_vector = CHUNKS[i]
+            for lo, hi, copy in ((0, by_vector, nc.vector.tensor_copy), (by_vector, width, nc.scalar.copy)):
                 if hi > lo:
-                    dstv = pairs[u][:, c0 + lo : c0 + hi].bitcast(BF16).rearrange("p (w j) -> p w j", j=2)
-                    copy(dstv, xf[i][:, :, lo:hi].rearrange("p j w -> p w j"))
+                    words = pairs[u][:, t0 + lo : t0 + hi].bitcast(BF16).rearrange("p (t j) -> p t j", j=2)
+                    copy(words, raw[i][:, :, lo:hi].rearrange("p j t -> p t j"))
 
-        start = {0: 4, 1: 6, 2: 3, 3: 5, 4: 2}
-        picked = {g: stage[:, 256 * start[g] : 256 * start[g] + 2 * n * BLK].rearrange("p (u s) -> p u s", u=2) for g, (b, n) in enumerate(GROUPS)}
+        picked = [
+            stage[:, REGION * r : REGION * r + 2 * n * BLK].rearrange("p (u s) -> p u s", u=2)
+            for r, (b0, n) in zip(FIRST_REGION, GROUPS)
+        ]
 
-        def gather(g, u, lo=0, hi=None):
-            b, n = GROUPS[g]
-            hi = n if hi is None else hi
-            cols = slice((b + lo) * BLK // 16, (b + hi) * BLK // 16)
+        def gather(g, u, lo, hi):
+            b0 = GROUPS[g][0]
+            cols = slice((b0 + lo) * BLK // LIST, (b0 + hi) * BLK // LIST)
             nc.vector.tensor_copy(picked[g][:, u, lo * BLK : hi * BLK], pairs[u][:].indirect(offs_sb[:, cols]))
 
-        codes, scales = {}, {}
+        def gather_group(g, u):
+            gather(g, u, 0, GROUPS[g][1])
 
-        def quantise(g):
-            b, n = GROUPS[g]
-            xg = keep.tile([P, n * BLK, 2], U32, name=f"xg{g}", align_bytes=256)
-            nc.scalar.copy(xg[:], picked[g].rearrange("p u s -> p s u"))
-            cd = keep.tile([P, n * BLK], U32, name=f"cd{b}", align_bytes=256)
-            sc = keep.tile([P, n * BLK], U8, name=f"sc{b}", align_bytes=256)
-            nc.vector.quantize_mx(out=cd[:].bitcast(FP8), scales=sc[:], in_=xg[:].rearrange("p s u -> p (s u)").bitcast(BF16))
+        x_codes, x_scales = {}, {}
+
+        def quantise_tokens(g):
+            b0, n = GROUPS[g]
+            woven = keep.tile([P, n * BLK, 2], U32, name=f"xg{g}", align_bytes=256)
+            nc.scalar.copy(woven[:], picked[g].rearrange("p u s -> p s u"))
+            codes = keep.tile([P, n * BLK], U32, name=f"cd{b0}", align_bytes=256)
+            scales = keep.tile([P, n * BLK], U8, name=f"sc{b0}", align_bytes=256)
+            nc.vector.quantize_mx(
+                out=codes[:].bitcast(FP8), scales=scales[:], in_=woven[:].rearrange("p s u -> p (s u)").bitcast(BF16)
+            )
             for i in range(n):
-                codes[b + i], scales[b + i] = cd[:, i * BLK : (i + 1) * BLK], sc[:, i * BLK : (i + 1) * BLK]
+                x_codes[b0 + i] = codes[:, i * BLK : (i + 1) * BLK]
+                x_scales[b0 + i] = scales[:, i * BLK : (i + 1) * BLK]
 
-        jz = keep.tile([P, 4 * H], BF16, name="jz", align_bytes=256)
-        jc = keep.tile([P, H], U32, name="jc", align_bytes=256)
-        js = keep.tile([P, H], U8, name="js", align_bytes=256)
-        nc.vector.memset(jz[:].bitcast(I32), 0)
-        nc.vector.quantize_mx(out=jc[:].bitcast(FP8), scales=js[:], in_=jz[:])
-        pw = psum.tile([P, H], F32, name="pt")
-        for i in range(4):
-            nc.tensor.matmul_mx(out=pw[:], lhsT=wt["w1", 0][:, 0:256].bitcast(FP4), lhsT_scale=js[:, 0:P], rhs=jc[:].bitcast(FP8), rhs_scale=js[:], start=True, stop=True)
+        zeros = keep.tile([P, 4 * H], BF16, name="jz", align_bytes=256)
+        zero_codes = keep.tile([P, H], U32, name="jc", align_bytes=256)
+        zero_scales = keep.tile([P, H], U8, name="js", align_bytes=256)
+        nc.vector.memset(zeros[:].bitcast(I32), 0)
+        nc.vector.quantize_mx(out=zero_codes[:].bitcast(FP8), scales=zero_scales[:], in_=zeros[:])
+        warm_sums = psum.tile([P, H], F32, name="pt")
+        for i in range(WARM_PASSES):
+            nc.tensor.matmul_mx(
+                out=warm_sums[:],
+                lhsT=weights["w1", 0][:, 0 : 2 * P].bitcast(FP4),
+                lhsT_scale=zero_scales[:, 0:P],
+                rhs=zero_codes[:].bitcast(FP8),
+                rhs_scale=zero_scales[:],
+                start=True,
+                stop=True,
+            )
+
         cast(0)
         cast(1)
-        w3s = keep.tile([P, E * H], U8, name="w3s", align_bytes=256, tag="xf1")
+        w3s = keep.tile([P, E * H], U8, name="w3s", align_bytes=256, tag=f"xf{W3_PLANE_CHUNK}")
         nc.vector.memset(w3s[:].bitcast(I32), 0)
-        for g in range(4):
-            gather(g, 0)
-        for i in (2, 3, 4):
+        for g in range(LAST_GROUP):
+            gather_group(g, 0)
+        for i in range(2, len(CHUNKS)):
             cast(i)
         load_scales(nc.scalar, w3s, w3_scales)
 
-        st = {}
+        silu_a, sums_b, h_turned, y_sb = {}, {}, {}, {}
 
         def project(b):
-            e = b // 2
+            e = b * BLK // C
             pa = psum.tile([P, H], F32, name="pa", bufs=2)
             pb = psum.tile([P, H], F32, name="pb", bufs=3)
-            for ps, key, plane in ((pa, "w1", w1s), (pb, "w3", w3s)):
+            for sums, key, plane in ((pa, "w1", w1s), (pb, "w3", w3s)):
                 nc.tensor.matmul_mx(
-                    out=ps[:],
-                    lhsT=codes[b].bitcast(FP8),
-                    lhsT_scale=scales[b],
-                    rhs=wt[key, e].bitcast(FP4),
+                    out=sums[:],
+                    lhsT=x_codes[b].bitcast(FP8),
+                    lhsT_scale=x_scales[b],
+                    rhs=weights[key, e].bitcast(FP4),
                     rhs_scale=plane[:, e * H : (e + 1) * H],
                     start=True,
                     stop=True,
                 )
             sil = work.tile([P, H], F32, name="sil", align_bytes=256)
             nc.scalar.activation(sil[:], pa[:], ACT.Silu)
-            st["sil", b], st["pb", b] = sil, pb
+            silu_a[b], sums_b[b] = sil, pb
 
         def product(b):
             h = work.tile([P, H], BF16, name="h", align_bytes=256)
-            nc.vector.tensor_tensor(h[:], st["sil", b][:], st["pb", b][:], MULT)
-            words = h[:].bitcast(F32)
+            nc.vector.tensor_tensor(h[:], silu_a[b][:], sums_b[b][:], MULT)
+            h_words = h[:].bitcast(F32)
             pt = psum.tile([P, 2, BLK], F32, name="pt")
             for u in range(2):
-                nc.tensor.transpose(pt[:, u, :], words[:, u : H // 2 : 2], ident[:])
+                nc.tensor.transpose(pt[:, u, :], h_words[:, u : H // 2 : 2], ident[:])
             hg = work.tile([P, BLK, 4], BF16, name="hg", align_bytes=256)
-            nc.scalar.copy(hg[:].rearrange("p s t -> p (s t)").bitcast(F32).rearrange("p (s u) -> p s u", u=2), pt[:].rearrange("p u s -> p s u"))
-            st["hg", b] = hg
+            hg_words = hg[:].rearrange("p s t -> p (s t)").bitcast(F32).rearrange("p (s u) -> p s u", u=2)
+            nc.scalar.copy(hg_words, pt[:].rearrange("p u s -> p s u"))
+            h_turned[b] = hg
 
         def down(b):
-            e = b // 2
+            e = b * BLK // C
             hc = work.tile([P, BLK], U32, name="hc", align_bytes=256)
             hs = work.tile([P, BLK], U8, name="hs", align_bytes=256)
-            nc.vector.quantize_mx(out=hc[:].bitcast(FP8), scales=hs[:], in_=st["hg", b][:].rearrange("p s t -> p (s t)"))
+            nc.vector.quantize_mx(out=hc[:].bitcast(FP8), scales=hs[:], in_=h_turned[b][:].rearrange("p s t -> p (s t)"))
             py = psum.tile([P, 2, BLK], F32, name="py", bufs=2)
             for m in range(2):
                 nc.tensor.matmul_mx(
                     out=py[:, m, :],
-                    lhsT=wt["w2", e][:, m * 256 : m * 256 + 256].bitcast(FP4),
-                    lhsT_scale=w2s[:, e * N + m * P : e * N + m * P + P],
+                    lhsT=weights["w2", e][:, 2 * m * P : 2 * (m + 1) * P].bitcast(FP4),
+                    lhsT_scale=w2s[:, e * N + m * P : e * N + (m + 1) * P],
                     rhs=hc[:].bitcast(FP8),
                     rhs_scale=hs[:],
                     start=True,
@@ -183,31 +210,30 @@ def tile_moe_two_glu_silu_kernel(
                 )
             ys = work.tile([P, 2, BLK], F32, name="ys", align_bytes=256)
             nc.scalar.copy(ys[:], py[:])
-            st["ys", b] = ys
+            y_sb[b] = ys
 
-        def place(b, m):
-            cols = slice(b * BLK // 16, (b + 1) * BLK // 16)
-            nc.vector.tensor_tensor(win[m][:].indirect(dst_sb[:, cols]), st["ys", b][:, m, :], gate_sb[:, b * BLK : (b + 1) * BLK], MULT)
+        def place(b):
+            cols = slice(b * BLK // LIST, (b + 1) * BLK // LIST)
+            for m in range(2):
+                nc.vector.tensor_tensor(
+                    win[m][:].indirect(dst_sb[:, cols]), y_sb[b][:, m, :], gate_sb[:, b * BLK : (b + 1) * BLK], MULT
+                )
 
-        first = {b: g for g, (b, n) in enumerate(GROUPS)}
-        gather(0, 1)
-        gather(1, 1)
-        gather(4, 0, 0, 1)
-        gather(4, 0, 1, 2)
-        for s in range(NBLK + 3):
-            if s in first:
-                g = first[s]
-                quantise(g)
-                if g + 2 < len(GROUPS):
-                    gather(g + 2, 1)
-            if s < NBLK:
-                project(s)
-            if 1 <= s <= NBLK:
-                product(s - 1)
-            if 2 <= s <= NBLK + 1:
-                down(s - 2)
-            if 3 <= s < NBLK + 3:
-                place(s - 3, 0)
-                place(s - 3, 1)
+        gather_group(0, 1)
+        gather_group(1, 1)
+        for i in range(GROUPS[LAST_GROUP][1]):
+            gather(LAST_GROUP, 0, i, i + 1)
+
+        group_from = {b0: g for g, (b0, n) in enumerate(GROUPS)}
+        stages = (project, product, down, place)
+        for step in range(NBLK + len(stages) - 1):
+            if step in group_from:
+                g = group_from[step]
+                quantise_tokens(g)
+                if g + 2 <= LAST_GROUP:
+                    gather_group(g + 2, 1)
+            for lag, stage_of_block in enumerate(stages):
+                if 0 <= step - lag < NBLK:
+                    stage_of_block(step - lag)
         for m in range(2):
             nc.sync.dma_start(out=out[m * P : (m + 1) * P, :], in_=win[m][:])

@@ -21,8 +21,6 @@ W3_PLANE_CHUNK = 1
 REGION = 256
 FIRST_REGION = (4, 6, 3, 5, 2)
 
-WARM_PASSES = 4
-
 F32 = mybir.dt.float32
 BF16 = mybir.dt.bfloat16
 I32 = mybir.dt.int32
@@ -132,23 +130,6 @@ def tile_moe_two_glu_silu_kernel(
             for i in range(n):
                 x_codes[b0 + i] = codes[:, i * BLK : (i + 1) * BLK]
                 x_scales[b0 + i] = scales[:, i * BLK : (i + 1) * BLK]
-
-        zeros = keep.tile([P, 4 * H], BF16, name="jz", align_bytes=256)
-        zero_codes = keep.tile([P, H], U32, name="jc", align_bytes=256)
-        zero_scales = keep.tile([P, H], U8, name="js", align_bytes=256)
-        nc.vector.memset(zeros[:].bitcast(I32), 0)
-        nc.vector.quantize_mx(out=zero_codes[:].bitcast(FP8), scales=zero_scales[:], in_=zeros[:])
-        warm_sums = psum.tile([P, H], F32, name="pt")
-        for i in range(WARM_PASSES):
-            nc.tensor.matmul_mx(
-                out=warm_sums[:],
-                lhsT=weights["w1", 0][:, 0 : 2 * P].bitcast(FP4),
-                lhsT_scale=zero_scales[:, 0:P],
-                rhs=zero_codes[:].bitcast(FP8),
-                rhs_scale=zero_scales[:],
-                start=True,
-                stop=True,
-            )
 
         cast(0)
         cast(1)

@@ -14,12 +14,13 @@ LIST = 16
 GROUPS = ((0, 1), (1, 1), (2, 2), (4, 2), (6, 2))
 LAST_GROUP = len(GROUPS) - 1
 
-CHUNKS = ((0, 0, 704, 704), (0, 704, 320, 224), (1, 0, 448, 0), (1, 448, 384, 0), (1, 832, 192, 192))
-STAGED_CHUNK = 3
-W3_PLANE_CHUNK = 1
+CHUNKS = ((0, 0, 704, 704), (0, 704, 320, 224), (1, 0, 256, 0), (1, 256, 320, 0), (1, 576, 320, 0), (1, 896, 128, 0))
 
 REGION = 256
-FIRST_REGION = (4, 6, 3, 5, 2)
+TURN_BANK = (0, 1, 0, 1, 1)
+Y_BANK = (1, 0, 1, 1, 0)
+WOVEN_TAG = ("xg0", "xg1", "xg2", "w3_0", "h1")
+FIRST_REGION = (0, 2, 4, 1, 3)
 
 F32 = mybir.dt.float32
 BF16 = mybir.dt.bfloat16
@@ -45,14 +46,15 @@ def tile_moe_two_glu_silu_kernel(
         offs_sb = keep.tile([P, E * C // LIST], U16, name="offs_sb")
         dst_sb = keep.tile([P, E * C // LIST], U16, name="dst_sb")
         w1s = keep.tile([P, E * H], U8, name="w1s", align_bytes=256)
+        w3s = keep.tile([P, E * H], U8, name="w3s", align_bytes=256)
         w2s = keep.tile([P, E * N], U8, name="w2s", align_bytes=256)
         pairs = [keep.tile([P, T], U32, name=f"pairs{u}", align_bytes=256) for u in range(2)]
         ident = keep.tile([P, P], F32, name="ident", align_bytes=256)
-        gate_sb = keep.tile([P, E * C], F32, name="gate_sb", align_bytes=256)
-        stage = keep.tile([P, 7 * REGION], U32, name="stage", align_bytes=256)
+        gate_sb = [keep.tile([P, E * C // 2], F32, name=f"gate{i}", align_bytes=256) for i in range(2)]
+        stage = keep.tile([P, 6 * REGION], U32, name="stage", align_bytes=256)
         win = [keep.tile([P, T], F32, name=f"win{m}", align_bytes=256) for m in range(2)]
 
-        for plane in (w1s, w2s):
+        for plane in (w1s, w3s, w2s):
             nc.vector.memset(plane[:].bitcast(I32), 0)
         table_warm = keep.tile([P, 1], F32, name="warm")
         nc.vector.memset(table_warm[:], 0.0)
@@ -67,10 +69,7 @@ def tile_moe_two_glu_silu_kernel(
         x_rows = xT.rearrange("(p j) t -> p j t", j=4)
         raw = []
         for i, (u, t0, width, by_vector) in enumerate(CHUNKS):
-            if i == STAGED_CHUNK:
-                chunk = stage[:, 0 : 2 * width].bitcast(F32).rearrange("p (j t) -> p j t", j=2)
-            else:
-                chunk = keep.tile([P, 2, width], F32, name=f"xf{i}", align_bytes=256, tag=f"xf{i}")[:]
+            chunk = keep.tile([P, 2, width], F32, name=f"xf{i}", align_bytes=256)[:]
             nc.sync.dma_start(out=chunk, in_=x_rows[:, 2 * u : 2 * u + 2, t0 : t0 + width])
             raw.append(chunk)
             if i == 0:
@@ -81,7 +80,7 @@ def tile_moe_two_glu_silu_kernel(
         weights = {}
 
         def load_words(key, src, e0, n):
-            tile = keep.tile([P, n, src.shape[3]], U8, name=f"{key}_{e0}", align_bytes=256)
+            tile = keep.tile([P, n, src.shape[3]], U8, name=f"{key}_{e0}", align_bytes=256, tag=f"{key}_{e0}")
             nc.sync.dma_start(out=tile[:].bitcast(I32), in_=src[e0 : e0 + n, 0].rearrange("e p b -> p e b").bitcast(I32))
             for i in range(n):
                 weights[key, e0 + i] = tile[:, i, :]
@@ -89,12 +88,15 @@ def tile_moe_two_glu_silu_kernel(
         load_words("w1", w1_words, 0, 1)
         load_scales(nc.sync, w1s, w1_scales)
         load_words("w3", w3_words, 0, 1)
+        load_scales(nc.sync, w2s, w2_scales)
+        load_scales(nc.sync, w3s, w3_scales)
         load_words("w1", w1_words, 1, E - 1)
         load_words("w3", w3_words, 1, E - 1)
         load_words("w2", w2_words, 0, E)
-        load_scales(nc.sync, w2s, w2_scales)
+        half = E * C // 2
         nc.sync.dma_start(dst_sb[:], dst)
-        nc.sync.dma_start(out=gate_sb[:], in_=gate[0:P, :])
+        nc.sync.dma_start(out=gate_sb[0][:], in_=gate[0:P, 0:half])
+        nc.sync.dma_start(out=gate_sb[1][:], in_=gate[0:P, half:])
 
         def cast(i):
             u, t0, width, by_vector = CHUNKS[i]
@@ -120,7 +122,7 @@ def tile_moe_two_glu_silu_kernel(
 
         def quantise_tokens(g):
             b0, n = GROUPS[g]
-            woven = keep.tile([P, n * BLK, 2], U32, name=f"xg{g}", align_bytes=256)
+            woven = keep.tile([P, n * BLK, 2], U32, name=f"xg{g}", align_bytes=256, tag=WOVEN_TAG[g])
             nc.scalar.copy(woven[:], picked[g].rearrange("p u s -> p s u"))
             codes = keep.tile([P, n * BLK], U32, name=f"cd{b0}", align_bytes=256)
             scales = keep.tile([P, n * BLK], U8, name=f"sc{b0}", align_bytes=256)
@@ -133,20 +135,18 @@ def tile_moe_two_glu_silu_kernel(
 
         cast(0)
         cast(1)
-        w3s = keep.tile([P, E * H], U8, name="w3s", align_bytes=256, tag=f"xf{W3_PLANE_CHUNK}")
-        nc.vector.memset(w3s[:].bitcast(I32), 0)
-        for g in range(LAST_GROUP):
+        for g in range(len(GROUPS)):
             gather_group(g, 0)
         for i in range(2, len(CHUNKS)):
             cast(i)
-        load_scales(nc.scalar, w3s, w3_scales)
 
-        silu_a, sums_b, h_turned, y_sb = {}, {}, {}, {}
+        silu_a, sums_b, h_rows, h_turned, y_sb = {}, {}, {}, {}, {}
+        bank = [psum.tile([P, 4 * BLK], F32, name=f"bank{i}") for i in range(2)]
 
         def project(b):
             e = b * BLK // C
             pa = psum.tile([P, H], F32, name="pa", bufs=2)
-            pb = psum.tile([P, H], F32, name="pb", bufs=3)
+            pb = psum.tile([P, H], F32, name="pb", bufs=4)
             for sums, key, plane in ((pa, "w1", w1s), (pb, "w3", w3s)):
                 nc.tensor.matmul_mx(
                     out=sums[:],
@@ -162,26 +162,39 @@ def tile_moe_two_glu_silu_kernel(
             silu_a[b], sums_b[b] = sil, pb
 
         def product(b):
-            h = work.tile([P, H], BF16, name="h", align_bytes=256)
+            h = keep.tile([P, H], BF16, name=f"h{b}", align_bytes=256, tag=f"h{b}")
             nc.vector.tensor_tensor(h[:], silu_a[b][:], sums_b[b][:], MULT)
-            h_words = h[:].bitcast(F32)
-            pt = psum.tile([P, 2, BLK], F32, name="pt")
-            for u in range(2):
-                nc.tensor.transpose(pt[:, u, :], h_words[:, u : H // 2 : 2], ident[:])
-            hg = work.tile([P, BLK, 4], BF16, name="hg", align_bytes=256)
-            hg_words = hg[:].rearrange("p s t -> p (s t)").bitcast(F32).rearrange("p (s u) -> p s u", u=2)
-            nc.scalar.copy(hg_words, pt[:].rearrange("p u s -> p s u"))
-            h_turned[b] = hg
+            h_rows[b] = h
 
-        def down(b):
-            e = b * BLK // C
-            hc = work.tile([P, BLK], U32, name="hc", align_bytes=256)
-            hs = work.tile([P, BLK], U8, name="hs", align_bytes=256)
-            nc.vector.quantize_mx(out=hc[:].bitcast(FP8), scales=hs[:], in_=h_turned[b][:].rearrange("p s t -> p (s t)"))
-            py = psum.tile([P, 2, BLK], F32, name="py", bufs=2)
+        def turn(g):
+            b0, n = GROUPS[g]
+            pt = bank[TURN_BANK[g]][:, 0 : 2 * n * BLK].rearrange("p (b u s) -> p b u s", b=n, u=2)
+            for i in range(n):
+                h_words = h_rows[b0 + i][:].bitcast(F32)
+                for u in range(2):
+                    nc.tensor.transpose(pt[:, i, u, :], h_words[:, u : H // 2 : 2], ident[:])
+            hg = keep.tile([P, n * BLK * 4], BF16, name=f"hg{g}", align_bytes=256)
+            hg_words = hg[:].bitcast(F32).rearrange("p (b s u) -> p b s u", b=n, u=2)
+            nc.scalar.copy(hg_words, pt.rearrange("p b u s -> p b s u"))
+            h_turned[g] = hg
+
+        h_codes = {}
+
+        def quantise_h(g):
+            b0, n = GROUPS[g]
+            hc = keep.tile([P, n * BLK], U32, name=f"hc{g}", align_bytes=256)
+            hs = keep.tile([P, n * BLK], U8, name=f"hs{g}", align_bytes=256)
+            nc.vector.quantize_mx(out=hc[:].bitcast(FP8), scales=hs[:], in_=h_turned[g][:])
+            h_codes[g] = (hc, hs)
+
+        def down(g):
+            b0, n = GROUPS[g]
+            e = b0 * BLK // C
+            hc, hs = h_codes[g]
+            py = bank[Y_BANK[g]][:, 0 : 2 * n * BLK]
             for m in range(2):
                 nc.tensor.matmul_mx(
-                    out=py[:, m, :],
+                    out=py[:, m * n * BLK : (m + 1) * n * BLK],
                     lhsT=weights["w2", e][:, 2 * m * P : 2 * (m + 1) * P].bitcast(FP4),
                     lhsT_scale=w2s[:, e * N + m * P : e * N + (m + 1) * P],
                     rhs=hc[:].bitcast(FP8),
@@ -189,32 +202,65 @@ def tile_moe_two_glu_silu_kernel(
                     start=True,
                     stop=True,
                 )
-            ys = work.tile([P, 2, BLK], F32, name="ys", align_bytes=256)
-            nc.scalar.copy(ys[:], py[:])
-            y_sb[b] = ys
+            ys = keep.tile([P, 2 * n * BLK], F32, name=f"ys{g}", align_bytes=256)
+            nc.scalar.copy(ys[:], py)
+            y_sb[g] = ys
 
-        def place(b):
-            cols = slice(b * BLK // LIST, (b + 1) * BLK // LIST)
+        def place(g):
+            b0, n = GROUPS[g]
+            cols = slice(b0 * BLK // LIST, (b0 + n) * BLK // LIST)
             for m in range(2):
                 nc.vector.tensor_tensor(
-                    win[m][:].indirect(dst_sb[:, cols]), y_sb[b][:, m, :], gate_sb[:, b * BLK : (b + 1) * BLK], MULT
+                    win[m][:].indirect(dst_sb[:, cols]),
+                    y_sb[g][:, m * n * BLK : (m + 1) * n * BLK],
+                    gate_sb[b0 * BLK // half][:, b0 * BLK % half : b0 * BLK % half + n * BLK],
+                    MULT,
                 )
 
-        gather_group(0, 1)
-        gather_group(1, 1)
-        for i in range(GROUPS[LAST_GROUP][1]):
-            gather(LAST_GROUP, 0, i, i + 1)
-
-        group_from = {b0: g for g, (b0, n) in enumerate(GROUPS)}
-        stages = (project, product, down, place)
-        for step in range(NBLK + len(stages) - 1):
-            if step in group_from:
-                g = group_from[step]
-                quantise_tokens(g)
-                if g + 2 <= LAST_GROUP:
-                    gather_group(g + 2, 1)
-            for lag, stage_of_block in enumerate(stages):
-                if 0 <= step - lag < NBLK:
-                    stage_of_block(step - lag)
+        for g in range(3):
+            gather_group(g, 1)
+        quantise_tokens(0)
+        quantise_tokens(1)
+        gather_group(3, 1)
+        project(0)
+        project(1)
+        quantise_tokens(2)
+        gather_group(4, 1)
+        product(0)
+        project(2)
+        product(1)
+        project(3)
+        turn(0)
+        turn(1)
+        quantise_tokens(3)
+        quantise_tokens(4)
+        quantise_h(0)
+        down(0)
+        product(2)
+        project(4)
+        quantise_h(1)
+        product(3)
+        turn(2)
+        project(5)
+        down(1)
+        place(0)
+        product(4)
+        project(6)
+        quantise_h(2)
+        product(5)
+        turn(3)
+        project(7)
+        down(2)
+        place(1)
+        product(6)
+        quantise_h(3)
+        product(7)
+        place(2)
+        turn(4)
+        down(3)
+        quantise_h(4)
+        down(4)
+        place(3)
+        place(4)
         for m in range(2):
             nc.sync.dma_start(out=out[m * P : (m + 1) * P, :], in_=win[m][:])

@@ -14,11 +14,12 @@ LIST = 16
 GROUPS = ((0, 1), (1, 1), (2, 2), (4, 2), (6, 2))
 LAST_GROUP = len(GROUPS) - 1
 
-CHUNKS = ((0, 0, 704, 704), (0, 704, 320, 224), (1, 0, 256, 0), (1, 256, 320, 0), (1, 576, 320, 0), (1, 896, 128, 0))
+CHUNKS = ((0, 0, 704, 704), (0, 704, 320, 224), (1, 0, 640, 0), (1, 640, 384, 256))
 
 REGION = 256
 TURN_BANK = (0, 1, 0, 1, 1)
-Y_BANK = (1, 0, 1, 1, 0)
+FIRST_ON_GPSIMD = 5
+H_TAG = ("h0", "h1", "h2", "h3", "h4", "hg2", "h6", "h7")
 WOVEN_TAG = ("xg0", "xg1", "xg2", "w3_0", "h1")
 FIRST_REGION = (0, 2, 4, 1, 3)
 
@@ -85,15 +86,17 @@ def tile_moe_two_glu_silu_kernel(
             for i in range(n):
                 weights[key, e0 + i] = tile[:, i, :]
 
+        half = E * C // 2
         load_words("w1", w1_words, 0, 1)
         load_scales(nc.sync, w1s, w1_scales)
         load_words("w3", w3_words, 0, 1)
         load_scales(nc.sync, w2s, w2_scales)
         load_scales(nc.sync, w3s, w3_scales)
-        load_words("w1", w1_words, 1, E - 1)
-        load_words("w3", w3_words, 1, E - 1)
+        load_words("w1", w1_words, 1, 1)
+        load_words("w3", w3_words, 1, 1)
         load_words("w2", w2_words, 0, E)
-        half = E * C // 2
+        load_words("w1", w1_words, 2, 2)
+        load_words("w3", w3_words, 2, 2)
         nc.sync.dma_start(dst_sb[:], dst)
         nc.sync.dma_start(out=gate_sb[0][:], in_=gate[0:P, 0:half])
         nc.sync.dma_start(out=gate_sb[1][:], in_=gate[0:P, half:])
@@ -160,10 +163,14 @@ def tile_moe_two_glu_silu_kernel(
             sil = work.tile([P, H], F32, name="sil", align_bytes=256)
             nc.scalar.activation(sil[:], pa[:], ACT.Silu)
             silu_a[b], sums_b[b] = sil, pb
+            if b >= FIRST_ON_GPSIMD:
+                sums_b[b] = work.tile([P, H], F32, name="b_sb", align_bytes=256)
+                nc.scalar.copy(sums_b[b][:], pb[:])
 
         def product(b):
-            h = keep.tile([P, H], BF16, name=f"h{b}", align_bytes=256, tag=f"h{b}")
-            nc.vector.tensor_tensor(h[:], silu_a[b][:], sums_b[b][:], MULT)
+            h = keep.tile([P, H], BF16, name=f"h{b}", align_bytes=256, tag=H_TAG[b])
+            eng = nc.vector if b < FIRST_ON_GPSIMD else nc.gpsimd
+            eng.tensor_tensor(h[:], silu_a[b][:], sums_b[b][:], MULT)
             h_rows[b] = h
 
         def turn(g):
@@ -173,7 +180,7 @@ def tile_moe_two_glu_silu_kernel(
                 h_words = h_rows[b0 + i][:].bitcast(F32)
                 for u in range(2):
                     nc.tensor.transpose(pt[:, i, u, :], h_words[:, u : H // 2 : 2], ident[:])
-            hg = keep.tile([P, n * BLK * 4], BF16, name=f"hg{g}", align_bytes=256)
+            hg = keep.tile([P, n * BLK * 4], BF16, name=f"hg{g}", align_bytes=256, tag=f"hg{g}")
             hg_words = hg[:].bitcast(F32).rearrange("p (b s u) -> p b s u", b=n, u=2)
             nc.scalar.copy(hg_words, pt.rearrange("p b u s -> p b s u"))
             h_turned[g] = hg
@@ -187,35 +194,55 @@ def tile_moe_two_glu_silu_kernel(
             nc.vector.quantize_mx(out=hc[:].bitcast(FP8), scales=hs[:], in_=h_turned[g][:])
             h_codes[g] = (hc, hs)
 
-        def down(g):
-            b0, n = GROUPS[g]
+        def down(g, lo, n, halves, sums, gate_now):
+            b0 = GROUPS[g][0] + lo
             e = b0 * BLK // C
             hc, hs = h_codes[g]
-            py = bank[Y_BANK[g]][:, 0 : 2 * n * BLK]
-            for m in range(2):
+            width = n * BLK
+            for i, m in enumerate(halves):
                 nc.tensor.matmul_mx(
-                    out=py[:, m * n * BLK : (m + 1) * n * BLK],
+                    out=sums[:, i * width : (i + 1) * width],
                     lhsT=weights["w2", e][:, 2 * m * P : 2 * (m + 1) * P].bitcast(FP4),
                     lhsT_scale=w2s[:, e * N + m * P : e * N + (m + 1) * P],
-                    rhs=hc[:].bitcast(FP8),
-                    rhs_scale=hs[:],
+                    rhs=hc[:, lo * BLK : lo * BLK + width].bitcast(FP8),
+                    rhs_scale=hs[:, lo * BLK : lo * BLK + width],
                     start=True,
                     stop=True,
                 )
-            ys = keep.tile([P, 2 * n * BLK], F32, name=f"ys{g}", align_bytes=256)
-            nc.scalar.copy(ys[:], py)
-            y_sb[g] = ys
+            ys = keep.tile([P, len(halves) * width], F32, name=f"ys{b0}_{halves[0]}", align_bytes=256)
+            gates = gate_sb[b0 * BLK // half][:, b0 * BLK % half : b0 * BLK % half + width]
+            if not gate_now:
+                nc.scalar.copy(ys[:], sums[:, 0 : len(halves) * width])
+            for i, m in enumerate(halves):
+                part = slice(i * width, (i + 1) * width)
+                if gate_now:
+                    nc.vector.tensor_tensor(ys[:, part], sums[:, part], gates, MULT)
+                y_sb[b0, m] = (ys[:, part], None if gate_now else gates, n)
 
-        def place(g):
-            b0, n = GROUPS[g]
-            cols = slice(b0 * BLK // LIST, (b0 + n) * BLK // LIST)
-            for m in range(2):
-                nc.vector.tensor_tensor(
-                    win[m][:].indirect(dst_sb[:, cols]),
-                    y_sb[g][:, m * n * BLK : (m + 1) * n * BLK],
-                    gate_sb[b0 * BLK // half][:, b0 * BLK % half : b0 * BLK % half + n * BLK],
-                    MULT,
-                )
+        def place(b0, m):
+            values, gates, n = y_sb[b0, m]
+            window = win[m][:].indirect(dst_sb[:, b0 * BLK // LIST : (b0 + n) * BLK // LIST])
+            if gates is None:
+                nc.vector.tensor_copy(window, values)
+            else:
+                nc.vector.tensor_tensor(window, values, gates, MULT)
+
+        zeros = keep.tile([P, 4 * BLK], BF16, name="zeros", align_bytes=256)
+        nc.vector.memset(zeros[:], 0.0)
+        zero_codes = keep.tile([P, BLK], U32, name="zero_codes", align_bytes=256)
+        zero_scales = keep.tile([P, H], U8, name="zero_scales", align_bytes=256)
+        nc.vector.memset(zero_scales[:].bitcast(I32), 0)
+        nc.vector.quantize_mx(out=zero_codes[:].bitcast(FP8), scales=zero_scales[:, 0:BLK], in_=zeros[:])
+        for i in range(4):
+            nc.tensor.matmul_mx(
+                out=bank[i % 2][:],
+                lhsT=zero_codes[:].bitcast(FP8),
+                lhsT_scale=zero_scales[:, 0:BLK],
+                rhs=weights["w1", 0].bitcast(FP4),
+                rhs_scale=zero_scales[:],
+                start=True,
+                stop=True,
+            )
 
         for g in range(3):
             gather_group(g, 1)
@@ -234,33 +261,44 @@ def tile_moe_two_glu_silu_kernel(
         turn(1)
         quantise_tokens(3)
         quantise_tokens(4)
-        quantise_h(0)
-        down(0)
         product(2)
-        project(4)
-        quantise_h(1)
         product(3)
+        quantise_h(0)
+        quantise_h(1)
+        both = (0, 1)
+        down(0, 0, 1, both, bank[1], False)
+        project(4)
         turn(2)
-        project(5)
-        down(1)
-        place(0)
         product(4)
-        project(6)
+        project(5)
+        place(0, 0)
+        place(0, 1)
         quantise_h(2)
         product(5)
-        turn(3)
-        project(7)
-        down(2)
-        place(1)
+        down(1, 0, 1, both, bank[0], True)
+        project(6)
         product(6)
-        quantise_h(3)
+        project(7)
         product(7)
-        place(2)
+        place(1, 0)
+        place(1, 1)
+        down(2, 0, 1, both, bank[0], True)
+        turn(3)
+        place(2, 0)
+        place(2, 1)
+        quantise_h(3)
+        down(2, 1, 1, both, bank[1], False)
+        down(3, 0, 2, (0,), bank[0], False)
         turn(4)
-        down(3)
+        place(3, 0)
+        place(3, 1)
+        place(4, 0)
         quantise_h(4)
-        down(4)
-        place(3)
-        place(4)
+        down(3, 0, 2, (1,), bank[1], False)
+        down(4, 0, 2, (0,), bank[0], False)
+        down(4, 0, 2, (1,), bank[1], False)
+        place(4, 1)
+        place(6, 0)
+        place(6, 1)
         for m in range(2):
             nc.sync.dma_start(out=out[m * P : (m + 1) * P, :], in_=win[m][:])

@@ -14,14 +14,17 @@ LIST = 16
 GROUPS = ((0, 1), (1, 1), (2, 2), (4, 2), (6, 2))
 LAST_GROUP = len(GROUPS) - 1
 
-CHUNKS = ((0, 0, 704, 704), (0, 704, 320, 224), (1, 0, 640, 0), (1, 640, 384, 256))
+CHUNKS = ((0, 0, 704, 704), (0, 704, 320, 224), (1, 0, 448, 0), (1, 448, 384, 0), (1, 832, 192, 192))
+STAGED_CHUNK = 3
+W3_PLANE_CHUNK = 1
 
 REGION = 256
+FIRST_REGION = (4, 6, 3, 5, 2)
 TURN_BANK = (0, 1, 0, 1, 1)
 FIRST_ON_GPSIMD = 5
+A_BANK = (2, 3, 2, 3, 2, 7, 3, 2)
+B_BANK = (4, 5, 6, 4, 5, 5, 4, 6)
 H_TAG = ("h0", "h1", "h2", "h3", "h4", "hg2", "h6", "h7")
-WOVEN_TAG = ("xg0", "xg1", "xg2", "w3_0", "h1")
-FIRST_REGION = (0, 2, 4, 1, 3)
 
 F32 = mybir.dt.float32
 BF16 = mybir.dt.bfloat16
@@ -47,21 +50,21 @@ def tile_moe_two_glu_silu_kernel(
         offs_sb = keep.tile([P, E * C // LIST], U16, name="offs_sb")
         dst_sb = keep.tile([P, E * C // LIST], U16, name="dst_sb")
         w1s = keep.tile([P, E * H], U8, name="w1s", align_bytes=256)
-        w3s = keep.tile([P, E * H], U8, name="w3s", align_bytes=256)
         w2s = keep.tile([P, E * N], U8, name="w2s", align_bytes=256)
         pairs = [keep.tile([P, T], U32, name=f"pairs{u}", align_bytes=256) for u in range(2)]
         ident = keep.tile([P, P], F32, name="ident", align_bytes=256)
-        gate_sb = [keep.tile([P, E * C // 2], F32, name=f"gate{i}", align_bytes=256) for i in range(2)]
-        stage = keep.tile([P, 6 * REGION], U32, name="stage", align_bytes=256)
+        half = E * C // 2
+        gate_sb = [keep.tile([P, half], F32, name=f"gate{i}", align_bytes=256) for i in range(2)]
+        stage = keep.tile([P, 7 * REGION], U32, name="stage", align_bytes=256)
         win = [keep.tile([P, T], F32, name=f"win{m}", align_bytes=256) for m in range(2)]
 
-        for plane in (w1s, w3s, w2s):
+        for plane in (w1s, w2s):
             nc.vector.memset(plane[:].bitcast(I32), 0)
         table_warm = keep.tile([P, 1], F32, name="warm")
         nc.vector.memset(table_warm[:], 0.0)
 
         def load_scales(eng, plane, src):
-            for q in range(4):
+            for q in (0, 2, 1, 3):
                 eng.dma_start(
                     out=plane[32 * q : 32 * q + 4, :].rearrange("r (e i) -> r e i", e=E).bitcast(I32),
                     in_=src[:, 0, 4 * q : 4 * q + 4, :].rearrange("e r i -> r e i").bitcast(I32),
@@ -70,7 +73,10 @@ def tile_moe_two_glu_silu_kernel(
         x_rows = xT.rearrange("(p j) t -> p j t", j=4)
         raw = []
         for i, (u, t0, width, by_vector) in enumerate(CHUNKS):
-            chunk = keep.tile([P, 2, width], F32, name=f"xf{i}", align_bytes=256)[:]
+            if i == STAGED_CHUNK:
+                chunk = stage[:, 0 : 2 * width].bitcast(F32).rearrange("p (j t) -> p j t", j=2)
+            else:
+                chunk = keep.tile([P, 2, width], F32, name=f"xf{i}", align_bytes=256, tag=f"xf{i}")[:]
             nc.sync.dma_start(out=chunk, in_=x_rows[:, 2 * u : 2 * u + 2, t0 : t0 + width])
             raw.append(chunk)
             if i == 0:
@@ -81,24 +87,22 @@ def tile_moe_two_glu_silu_kernel(
         weights = {}
 
         def load_words(key, src, e0, n):
-            tile = keep.tile([P, n, src.shape[3]], U8, name=f"{key}_{e0}", align_bytes=256, tag=f"{key}_{e0}")
+            tile = keep.tile([P, n, src.shape[3]], U8, name=f"{key}_{e0}", align_bytes=256)
             nc.sync.dma_start(out=tile[:].bitcast(I32), in_=src[e0 : e0 + n, 0].rearrange("e p b -> p e b").bitcast(I32))
             for i in range(n):
                 weights[key, e0 + i] = tile[:, i, :]
 
-        half = E * C // 2
         load_words("w1", w1_words, 0, 1)
         load_scales(nc.sync, w1s, w1_scales)
         load_words("w3", w3_words, 0, 1)
-        load_scales(nc.sync, w2s, w2_scales)
-        load_scales(nc.sync, w3s, w3_scales)
-        load_words("w1", w1_words, 1, 1)
-        load_words("w3", w3_words, 1, 1)
+        load_words("w1", w1_words, 1, 2)
+        load_words("w3", w3_words, 1, 2)
         load_words("w2", w2_words, 0, E)
-        load_words("w1", w1_words, 2, 2)
-        load_words("w3", w3_words, 2, 2)
+        load_scales(nc.sync, w2s, w2_scales)
         nc.sync.dma_start(dst_sb[:], dst)
         nc.sync.dma_start(out=gate_sb[0][:], in_=gate[0:P, 0:half])
+        load_words("w1", w1_words, 3, 1)
+        load_words("w3", w3_words, 3, 1)
         nc.sync.dma_start(out=gate_sb[1][:], in_=gate[0:P, half:])
 
         def cast(i):
@@ -125,7 +129,7 @@ def tile_moe_two_glu_silu_kernel(
 
         def quantise_tokens(g):
             b0, n = GROUPS[g]
-            woven = keep.tile([P, n * BLK, 2], U32, name=f"xg{g}", align_bytes=256, tag=WOVEN_TAG[g])
+            woven = keep.tile([P, n * BLK, 2], U32, name=f"xg{g}", align_bytes=256)
             nc.scalar.copy(woven[:], picked[g].rearrange("p u s -> p s u"))
             codes = keep.tile([P, n * BLK], U32, name=f"cd{b0}", align_bytes=256)
             scales = keep.tile([P, n * BLK], U8, name=f"sc{b0}", align_bytes=256)
@@ -138,18 +142,28 @@ def tile_moe_two_glu_silu_kernel(
 
         cast(0)
         cast(1)
-        for g in range(len(GROUPS)):
+        w3s = keep.tile([P, E * H], U8, name="w3s", align_bytes=256, tag=f"xf{W3_PLANE_CHUNK}")
+        nc.vector.memset(w3s[:].bitcast(I32), 0)
+        for g in range(LAST_GROUP):
             gather_group(g, 0)
         for i in range(2, len(CHUNKS)):
             cast(i)
+        load_scales(nc.scalar, w3s, w3_scales)
 
         silu_a, sums_b, h_rows, h_turned, y_sb = {}, {}, {}, {}, {}
-        bank = [psum.tile([P, 4 * BLK], F32, name=f"bank{i}") for i in range(2)]
+        bank = [psum.tile([P, 4 * BLK], F32, name=f"bank{i}") for i in range(8)]
+
+        shared = keep.tile([P, 3 * C], F32, name="shared", align_bytes=256)
+
+        def by_pair(sums):
+            return sums[:].rearrange("s (q u d) -> s u q d", u=2, d=2)
+
+        def in_halves(tile):
+            return tile[:].rearrange("s (u q d) -> s u q d", u=2, d=2)
 
         def project(b):
             e = b * BLK // C
-            pa = psum.tile([P, H], F32, name="pa", bufs=2)
-            pb = psum.tile([P, H], F32, name="pb", bufs=4)
+            pa, pb = bank[A_BANK[b]], bank[B_BANK[b]]
             for sums, key, plane in ((pa, "w1", w1s), (pb, "w3", w3s)):
                 nc.tensor.matmul_mx(
                     out=sums[:],
@@ -161,16 +175,22 @@ def tile_moe_two_glu_silu_kernel(
                     stop=True,
                 )
             sil = work.tile([P, H], F32, name="sil", align_bytes=256)
-            nc.scalar.activation(sil[:], pa[:], ACT.Silu)
-            silu_a[b], sums_b[b] = sil, pb
+            nc.scalar.activation(in_halves(sil), by_pair(pa), ACT.Silu)
+            silu_a[b], sums_b[b] = in_halves(sil), by_pair(pb)
             if b >= FIRST_ON_GPSIMD:
-                sums_b[b] = work.tile([P, H], F32, name="b_sb", align_bytes=256)
-                nc.scalar.copy(sums_b[b][:], pb[:])
+                b_sb = work.tile([P, H], F32, name="b_sb", align_bytes=256)
+                nc.scalar.copy(in_halves(b_sb), sums_b[b])
+                silu_a[b], sums_b[b] = sil[:], b_sb[:]
 
         def product(b):
-            h = keep.tile([P, H], BF16, name=f"h{b}", align_bytes=256, tag=H_TAG[b])
-            eng = nc.vector if b < FIRST_ON_GPSIMD else nc.gpsimd
-            eng.tensor_tensor(h[:], silu_a[b][:], sums_b[b][:], MULT)
+            if b == FIRST_ON_GPSIMD:
+                h = shared[:, 3 * BLK : 5 * BLK].bitcast(BF16)
+            else:
+                h = keep.tile([P, H], BF16, name=f"h{b}", align_bytes=256, tag=f"h{b}")[:]
+            if b < FIRST_ON_GPSIMD:
+                nc.vector.tensor_tensor(in_halves(h), silu_a[b], sums_b[b], MULT)
+            else:
+                nc.gpsimd.tensor_tensor(h, silu_a[b], sums_b[b], MULT)
             h_rows[b] = h
 
         def turn(g):
@@ -179,8 +199,11 @@ def tile_moe_two_glu_silu_kernel(
             for i in range(n):
                 h_words = h_rows[b0 + i][:].bitcast(F32)
                 for u in range(2):
-                    nc.tensor.transpose(pt[:, i, u, :], h_words[:, u : H // 2 : 2], ident[:])
-            hg = keep.tile([P, n * BLK * 4], BF16, name=f"hg{g}", align_bytes=256, tag=f"hg{g}")
+                    nc.tensor.transpose(pt[:, i, u, :], h_words[:, u * P : (u + 1) * P], ident[:])
+            if g == 2:
+                hg = shared[:, 0 : 2 * C].bitcast(BF16)
+            else:
+                hg = keep.tile([P, n * BLK * 4], BF16, name=f"hg{g}", align_bytes=256)[:]
             hg_words = hg[:].bitcast(F32).rearrange("p (b s u) -> p b s u", b=n, u=2)
             nc.scalar.copy(hg_words, pt.rearrange("p b u s -> p b s u"))
             h_turned[g] = hg
@@ -194,7 +217,7 @@ def tile_moe_two_glu_silu_kernel(
             nc.vector.quantize_mx(out=hc[:].bitcast(FP8), scales=hs[:], in_=h_turned[g][:])
             h_codes[g] = (hc, hs)
 
-        def down(g, lo, n, halves, sums, gate_now):
+        def down(g, lo, n, halves, sums, gate_now, tag=None):
             b0 = GROUPS[g][0] + lo
             e = b0 * BLK // C
             hc, hs = h_codes[g]
@@ -209,7 +232,10 @@ def tile_moe_two_glu_silu_kernel(
                     start=True,
                     stop=True,
                 )
-            ys = keep.tile([P, len(halves) * width], F32, name=f"ys{b0}_{halves[0]}", align_bytes=256)
+            if b0 == 0:
+                ys = shared[:, 2 * C : 3 * C]
+            else:
+                ys = keep.tile([P, len(halves) * width], F32, name=f"ys{b0}", align_bytes=256, tag=tag or f"ys{b0}")[:]
             gates = gate_sb[b0 * BLK // half][:, b0 * BLK % half : b0 * BLK % half + width]
             if not gate_now:
                 nc.scalar.copy(ys[:], sums[:, 0 : len(halves) * width])
@@ -244,29 +270,32 @@ def tile_moe_two_glu_silu_kernel(
                 stop=True,
             )
 
-        for g in range(3):
-            gather_group(g, 1)
+        gather_group(0, 1)
+        gather_group(1, 1)
+        for i in range(GROUPS[LAST_GROUP][1]):
+            gather(LAST_GROUP, 0, i, i + 1)
         quantise_tokens(0)
+        gather_group(2, 1)
+        project(0)
         quantise_tokens(1)
         gather_group(3, 1)
-        project(0)
         project(1)
+        product(0)
+        turn(0)
         quantise_tokens(2)
         gather_group(4, 1)
-        product(0)
         project(2)
         product(1)
-        project(3)
-        turn(0)
         turn(1)
-        quantise_tokens(3)
-        quantise_tokens(4)
-        product(2)
-        product(3)
         quantise_h(0)
+        project(3)
+        product(2)
+        quantise_tokens(3)
         quantise_h(1)
+        product(3)
+        quantise_tokens(4)
         both = (0, 1)
-        down(0, 0, 1, both, bank[1], False)
+        down(0, 0, 1, both, bank[7], False)
         project(4)
         turn(2)
         product(4)
@@ -287,16 +316,14 @@ def tile_moe_two_glu_silu_kernel(
         place(2, 0)
         place(2, 1)
         quantise_h(3)
-        down(2, 1, 1, both, bank[1], False)
-        down(3, 0, 2, (0,), bank[0], False)
+        down(2, 1, 1, both, bank[0], False, "h4")
         turn(4)
+        down(3, 0, 2, both, bank[0], False, "h7")
         place(3, 0)
         place(3, 1)
-        place(4, 0)
         quantise_h(4)
-        down(3, 0, 2, (1,), bank[1], False)
-        down(4, 0, 2, (0,), bank[0], False)
-        down(4, 0, 2, (1,), bank[1], False)
+        down(4, 0, 2, both, bank[1], False)
+        place(4, 0)
         place(4, 1)
         place(6, 0)
         place(6, 1)

@@ -253,23 +253,6 @@ def tile_moe_two_glu_silu_kernel(
             else:
                 nc.vector.tensor_tensor(window, values, gates, MULT)
 
-        zeros = keep.tile([P, 4 * BLK], BF16, name="zeros", align_bytes=256)
-        nc.vector.memset(zeros[:], 0.0)
-        zero_codes = keep.tile([P, BLK], U32, name="zero_codes", align_bytes=256)
-        zero_scales = keep.tile([P, H], U8, name="zero_scales", align_bytes=256)
-        nc.vector.memset(zero_scales[:].bitcast(I32), 0)
-        nc.vector.quantize_mx(out=zero_codes[:].bitcast(FP8), scales=zero_scales[:, 0:BLK], in_=zeros[:])
-        for i in range(4):
-            nc.tensor.matmul_mx(
-                out=bank[i % 2][:],
-                lhsT=zero_codes[:].bitcast(FP8),
-                lhsT_scale=zero_scales[:, 0:BLK],
-                rhs=weights["w1", 0].bitcast(FP4),
-                rhs_scale=zero_scales[:],
-                start=True,
-                stop=True,
-            )
-
         gather_group(0, 1)
         gather_group(1, 1)
         for i in range(GROUPS[LAST_GROUP][1]):

@@ -7,24 +7,21 @@ K, T, E, C, H, N = 512, 1024, 4, 256, 512, 256
 FLOPS = 2 * E * C * (K * H + K * H + H * N)
 
 P = 128
-BLK = 128
-NBLK = E * C // BLK
+SLAB = 128
 LIST = 16
+WORD = 2
+NEIGHBOURS = 4
 
-GROUPS = ((0, 1), (1, 1), (2, 2), (4, 2), (6, 2))
-LAST_GROUP = len(GROUPS) - 1
+CHUNKS = ((0, 512, 320), (512, 320, 128), (832, 192, 128))
+RUN = 256
 
-CHUNKS = ((0, 0, 704, 704), (0, 704, 320, 224), (1, 0, 448, 0), (1, 448, 384, 0), (1, 832, 192, 192))
-STAGED_CHUNK = 3
-W3_PLANE_CHUNK = 1
+FIRST_ON_GPSIMD = 3
 
-REGION = 256
-FIRST_REGION = (4, 6, 3, 5, 2)
-TURN_BANK = (0, 1, 0, 1, 1)
-FIRST_ON_GPSIMD = 5
-A_BANK = (2, 3, 2, 3, 2, 7, 3, 2)
-B_BANK = (4, 5, 6, 4, 5, 5, 4, 6)
-H_TAG = ("h0", "h1", "h2", "h3", "h4", "hg2", "h6", "h7")
+A_BANK = (2, 3, 2, 3, 2, 3, 2, 3)
+B_BANK = (4, 5, 6, 5, 4, 6, 5, 4)
+TURN_BANK = (0, 1, 0, 0, 6, 6, 0, 0)
+FIRST_Y_BANK = 7
+LAST_Y_BANKS = (2, 3, 4, 5)
 
 F32 = mybir.dt.float32
 BF16 = mybir.dt.bfloat16
@@ -44,271 +41,257 @@ def tile_moe_two_glu_silu_kernel(
     nc = tc.nc
     with ExitStack() as ctx:
         keep = ctx.enter_context(tc.tile_pool(name="keep", bufs=1))
-        work = ctx.enter_context(tc.tile_pool(name="work", bufs=NBLK))
         psum = ctx.enter_context(tc.psum_pool(name="psum", bufs=1))
+
+        def sbuf(name, columns, dtype, takes_over=None):
+            return keep.tile([P, columns], dtype, name=name, align_bytes=256, tag=takes_over or name)[:]
 
         offs_sb = keep.tile([P, E * C // LIST], U16, name="offs_sb")
         dst_sb = keep.tile([P, E * C // LIST], U16, name="dst_sb")
-        w1s = keep.tile([P, E * H], U8, name="w1s", align_bytes=256)
-        w2s = keep.tile([P, E * N], U8, name="w2s", align_bytes=256)
-        pairs = [keep.tile([P, T], U32, name=f"pairs{u}", align_bytes=256) for u in range(2)]
-        ident = keep.tile([P, P], F32, name="ident", align_bytes=256)
-        half = E * C // 2
-        gate_sb = [keep.tile([P, half], F32, name=f"gate{i}", align_bytes=256) for i in range(2)]
-        stage = keep.tile([P, 7 * REGION], U32, name="stage", align_bytes=256)
-        win = [keep.tile([P, T], F32, name=f"win{m}", align_bytes=256) for m in range(2)]
+        w1_plane = sbuf("w1_plane", E * H, U8)
+        w3_plane = sbuf("w3_plane", E * H, U8)
+        w2_plane = sbuf("w2_plane", E * N, U8)
+        rounded = sbuf("rounded", 4 * T, BF16)
+        token_codes = sbuf("token_codes", T, U32)
+        token_plane = sbuf("token_plane", T, U8)
+        ident = sbuf("ident", P, F32)
+        half_slots = E * C // 2
+        gate_sb = [sbuf(f"gate{i}", half_slots, F32) for i in range(2)]
+        bank = [psum.tile([P, 4 * SLAB], F32, name=f"bank{i}") for i in range(8)]
 
-        for plane in (w1s, w2s):
-            nc.vector.memset(plane[:].bitcast(I32), 0)
-        table_warm = keep.tile([P, 1], F32, name="warm")
+        for plane in (w1_plane, w3_plane, w2_plane, token_plane):
+            nc.vector.memset(plane.bitcast(I32), 0)
+        table_warm = keep.tile([P, 1], F32, name="table_warm")
         nc.vector.memset(table_warm[:], 0.0)
 
-        def load_scales(eng, plane, src):
+        def load_scales(plane, src):
             for q in (0, 2, 1, 3):
-                eng.dma_start(
+                nc.sync.dma_start(
                     out=plane[32 * q : 32 * q + 4, :].rearrange("r (e i) -> r e i", e=E).bitcast(I32),
                     in_=src[:, 0, 4 * q : 4 * q + 4, :].rearrange("e r i -> r e i").bitcast(I32),
                 )
 
         x_rows = xT.rearrange("(p j) t -> p j t", j=4)
         raw = []
-        for i, (u, t0, width, by_vector) in enumerate(CHUNKS):
-            if i == STAGED_CHUNK:
-                chunk = stage[:, 0 : 2 * width].bitcast(F32).rearrange("p (j t) -> p j t", j=2)
-            else:
-                chunk = keep.tile([P, 2, width], F32, name=f"xf{i}", align_bytes=256, tag=f"xf{i}")[:]
-            nc.sync.dma_start(out=chunk, in_=x_rows[:, 2 * u : 2 * u + 2, t0 : t0 + width])
+        for i, (t0, width, by_vector) in enumerate(CHUNKS):
+            chunk = keep.tile([P, 4, width], F32, name=f"raw{i}", align_bytes=256)[:]
+            nc.sync.dma_start(out=chunk, in_=x_rows[:, :, t0 : t0 + width])
             raw.append(chunk)
-            if i == 0:
-                nc.sync.dma_start(offs_sb[:], offs)
+        nc.sync.dma_start(offs_sb[:], offs)
         nc.scalar.activation(table_warm[:], table_warm[:], ACT.Silu)
-        make_identity(nc, ident[:])
+        make_identity(nc, ident)
 
         weights = {}
 
         def load_words(key, src, e0, n):
-            tile = keep.tile([P, n, src.shape[3]], U8, name=f"{key}_{e0}", align_bytes=256)
-            nc.sync.dma_start(out=tile[:].bitcast(I32), in_=src[e0 : e0 + n, 0].rearrange("e p b -> p e b").bitcast(I32))
+            rows = sbuf(f"{key}_words{e0}", n * src.shape[3], U8).rearrange("p (e b) -> p e b", e=n)
+            nc.sync.dma_start(out=rows.bitcast(I32), in_=src[e0 : e0 + n, 0].rearrange("e p b -> p e b").bitcast(I32))
             for i in range(n):
-                weights[key, e0 + i] = tile[:, i, :]
+                weights[key, e0 + i] = rows[:, i, :]
 
         load_words("w1", w1_words, 0, 1)
-        load_scales(nc.sync, w1s, w1_scales)
+        load_scales(w1_plane, w1_scales)
+        load_scales(w2_plane, w2_scales)
         load_words("w3", w3_words, 0, 1)
-        load_words("w1", w1_words, 1, 2)
-        load_words("w3", w3_words, 1, 2)
+        load_scales(w3_plane, w3_scales)
+        for e0, n in ((1, 1), (2, E - 2)):
+            load_words("w1", w1_words, e0, n)
+            load_words("w3", w3_words, e0, n)
         load_words("w2", w2_words, 0, E)
-        load_scales(nc.sync, w2s, w2_scales)
+        nc.sync.dma_start(out=gate_sb[0], in_=gate[0:P, 0:half_slots])
         nc.sync.dma_start(dst_sb[:], dst)
-        nc.sync.dma_start(out=gate_sb[0][:], in_=gate[0:P, 0:half])
-        load_words("w1", w1_words, 3, 1)
-        load_words("w3", w3_words, 3, 1)
-        nc.sync.dma_start(out=gate_sb[1][:], in_=gate[0:P, half:])
+        nc.sync.dma_start(out=gate_sb[1], in_=gate[0:P, half_slots:])
 
         def cast(i):
-            u, t0, width, by_vector = CHUNKS[i]
+            t0, width, by_vector = CHUNKS[i]
             for lo, hi, copy in ((0, by_vector, nc.vector.tensor_copy), (by_vector, width, nc.scalar.copy)):
-                if hi > lo:
-                    words = pairs[u][:, t0 + lo : t0 + hi].bitcast(BF16).rearrange("p (t j) -> p t j", j=2)
-                    copy(words, raw[i][:, :, lo:hi].rearrange("p j t -> p t j"))
+                values = rounded[:, 4 * (t0 + lo) : 4 * (t0 + hi)].rearrange("p (c t j) -> p c j t", t=NEIGHBOURS, j=4)
+                copy(values, raw[i][:, :, lo:hi].rearrange("p j (c t) -> p c j t", t=NEIGHBOURS))
 
-        picked = [
-            stage[:, REGION * r : REGION * r + 2 * n * BLK].rearrange("p (u s) -> p u s", u=2)
-            for r, (b0, n) in zip(FIRST_REGION, GROUPS)
-        ]
-
-        def gather(g, u, lo, hi):
-            b0 = GROUPS[g][0]
-            cols = slice((b0 + lo) * BLK // LIST, (b0 + hi) * BLK // LIST)
-            nc.vector.tensor_copy(picked[g][:, u, lo * BLK : hi * BLK], pairs[u][:].indirect(offs_sb[:, cols]))
-
-        def gather_group(g, u):
-            gather(g, u, 0, GROUPS[g][1])
+        def quantise_tokens(r):
+            tokens = slice(r * RUN, (r + 1) * RUN)
+            nc.vector.quantize_mx(
+                out=token_codes[:, tokens].bitcast(FP8),
+                scales=token_plane[:, tokens],
+                in_=rounded[:, 4 * r * RUN : 4 * (r + 1) * RUN],
+            )
 
         x_codes, x_scales = {}, {}
 
-        def quantise_tokens(g):
-            b0, n = GROUPS[g]
-            woven = keep.tile([P, n * BLK, 2], U32, name=f"xg{g}", align_bytes=256)
-            nc.scalar.copy(woven[:], picked[g].rearrange("p u s -> p s u"))
-            codes = keep.tile([P, n * BLK], U32, name=f"cd{b0}", align_bytes=256)
-            scales = keep.tile([P, n * BLK], U8, name=f"sc{b0}", align_bytes=256)
-            nc.vector.quantize_mx(
-                out=codes[:].bitcast(FP8), scales=scales[:], in_=woven[:].rearrange("p s u -> p (s u)").bitcast(BF16)
-            )
+        def gather(name, dtype, window, found, s0, n, takes_over):
+            picked = sbuf(f"{name}{s0}", n * SLAB, dtype, takes_over)
+            nc.vector.tensor_copy(picked, window.indirect(offs_sb[:, s0 * SLAB // LIST : (s0 + n) * SLAB // LIST]))
             for i in range(n):
-                x_codes[b0 + i] = codes[:, i * BLK : (i + 1) * BLK]
-                x_scales[b0 + i] = scales[:, i * BLK : (i + 1) * BLK]
+                found[s0 + i] = picked[:, i * SLAB : (i + 1) * SLAB]
 
-        cast(0)
-        cast(1)
-        w3s = keep.tile([P, E * H], U8, name="w3s", align_bytes=256, tag=f"xf{W3_PLANE_CHUNK}")
-        nc.vector.memset(w3s[:].bitcast(I32), 0)
-        for g in range(LAST_GROUP):
-            gather_group(g, 0)
-        for i in range(2, len(CHUNKS)):
-            cast(i)
-        load_scales(nc.scalar, w3s, w3_scales)
+        def gather_codes(s0, n, takes_over=None):
+            gather("x_codes", U32, token_codes, x_codes, s0, n, takes_over)
 
-        silu_a, sums_b, h_rows, h_turned, y_sb = {}, {}, {}, {}, {}
-        bank = [psum.tile([P, 4 * BLK], F32, name=f"bank{i}") for i in range(8)]
+        def gather_scales(s0, n, takes_over=None):
+            gather("x_scales", U8, token_plane, x_scales, s0, n, takes_over)
 
-        shared = keep.tile([P, 3 * C], F32, name="shared", align_bytes=256)
+        silu_a, sums_b, h_rows, h_turned, y_sums, y_rows, window = {}, {}, {}, {}, {}, {}, {}
 
         def by_pair(sums):
             return sums[:].rearrange("s (q u d) -> s u q d", u=2, d=2)
 
-        def in_halves(tile):
-            return tile[:].rearrange("s (u q d) -> s u q d", u=2, d=2)
+        def in_pair_order(tile):
+            return tile.rearrange("s (u q d) -> s u q d", u=2, d=2)
 
-        def project(b):
-            e = b * BLK // C
-            pa, pb = bank[A_BANK[b]], bank[B_BANK[b]]
-            for sums, key, plane in ((pa, "w1", w1s), (pb, "w3", w3s)):
+        def project(s):
+            e = s * SLAB // C
+            pa, pb = bank[A_BANK[s]], bank[B_BANK[s]]
+            for sums, key, plane in ((pa, "w1", w1_plane), (pb, "w3", w3_plane)):
                 nc.tensor.matmul_mx(
                     out=sums[:],
-                    lhsT=x_codes[b].bitcast(FP8),
-                    lhsT_scale=x_scales[b],
+                    lhsT=x_codes[s].bitcast(FP8),
+                    lhsT_scale=x_scales[s],
                     rhs=weights[key, e].bitcast(FP4),
                     rhs_scale=plane[:, e * H : (e + 1) * H],
                     start=True,
                     stop=True,
                 )
-            sil = work.tile([P, H], F32, name="sil", align_bytes=256)
-            nc.scalar.activation(in_halves(sil), by_pair(pa), ACT.Silu)
-            silu_a[b], sums_b[b] = in_halves(sil), by_pair(pb)
-            if b >= FIRST_ON_GPSIMD:
-                b_sb = work.tile([P, H], F32, name="b_sb", align_bytes=256)
-                nc.scalar.copy(in_halves(b_sb), sums_b[b])
-                silu_a[b], sums_b[b] = sil[:], b_sb[:]
-
-        def product(b):
-            if b == FIRST_ON_GPSIMD:
-                h = shared[:, 3 * BLK : 5 * BLK].bitcast(BF16)
+            silu_a[s] = sbuf(f"silu{s}", H, F32)
+            nc.scalar.activation(in_pair_order(silu_a[s]), by_pair(pa), ACT.Silu)
+            if s < FIRST_ON_GPSIMD:
+                sums_b[s] = by_pair(pb)
             else:
-                h = keep.tile([P, H], BF16, name=f"h{b}", align_bytes=256, tag=f"h{b}")[:]
-            if b < FIRST_ON_GPSIMD:
-                nc.vector.tensor_tensor(in_halves(h), silu_a[b], sums_b[b], MULT)
+                sums_b[s] = sbuf(f"b{s}", H, F32)
+                nc.scalar.copy(in_pair_order(sums_b[s]), by_pair(pb))
+
+        def product(s, takes_over=None):
+            h_rows[s] = sbuf(f"h{s}", H, BF16, takes_over)
+            if s < FIRST_ON_GPSIMD:
+                nc.vector.tensor_tensor(in_pair_order(h_rows[s]), in_pair_order(silu_a[s]), sums_b[s], MULT)
             else:
-                nc.gpsimd.tensor_tensor(h, silu_a[b], sums_b[b], MULT)
-            h_rows[b] = h
+                nc.gpsimd.tensor_tensor(h_rows[s], silu_a[s], sums_b[s], MULT)
 
-        def turn(g):
-            b0, n = GROUPS[g]
-            pt = bank[TURN_BANK[g]][:, 0 : 2 * n * BLK].rearrange("p (b u s) -> p b u s", b=n, u=2)
-            for i in range(n):
-                h_words = h_rows[b0 + i][:].bitcast(F32)
-                for u in range(2):
-                    nc.tensor.transpose(pt[:, i, u, :], h_words[:, u * P : (u + 1) * P], ident[:])
-            if g == 2:
-                hg = shared[:, 0 : 2 * C].bitcast(BF16)
-            else:
-                hg = keep.tile([P, n * BLK * 4], BF16, name=f"hg{g}", align_bytes=256)[:]
-            hg_words = hg[:].bitcast(F32).rearrange("p (b s u) -> p b s u", b=n, u=2)
-            nc.scalar.copy(hg_words, pt.rearrange("p b u s -> p b s u"))
-            h_turned[g] = hg
+        def turn_columns(s, n):
+            side = s % 2 if s > 1 else 0
+            columns = bank[TURN_BANK[s]][:, 2 * side * SLAB : 2 * (side + n) * SLAB]
+            return columns.rearrange("p (b u s) -> p b u s", b=n, u=2)
 
-        h_codes = {}
+        def turn(s):
+            h_words = h_rows[s].bitcast(F32)
+            for u in range(2):
+                nc.tensor.transpose(turn_columns(s, 1)[:, 0, u, :], h_words[:, u * P : (u + 1) * P], ident)
 
-        def quantise_h(g):
-            b0, n = GROUPS[g]
-            hc = keep.tile([P, n * BLK], U32, name=f"hc{g}", align_bytes=256)
-            hs = keep.tile([P, n * BLK], U8, name=f"hs{g}", align_bytes=256)
-            nc.vector.quantize_mx(out=hc[:].bitcast(FP8), scales=hs[:], in_=h_turned[g][:])
-            h_codes[g] = (hc, hs)
+        def collect(s, n):
+            h_turned[s] = sbuf(f"turned{s}", n * SLAB * 4, BF16)
+            words = h_turned[s].bitcast(F32).rearrange("p (b s u) -> p b s u", b=n, u=2)
+            nc.scalar.copy(words, turn_columns(s, n).rearrange("p b u s -> p b s u"))
 
-        def down(g, lo, n, halves, sums, gate_now, tag=None):
-            b0 = GROUPS[g][0] + lo
-            e = b0 * BLK // C
-            hc, hs = h_codes[g]
-            width = n * BLK
-            for i, m in enumerate(halves):
-                nc.tensor.matmul_mx(
-                    out=sums[:, i * width : (i + 1) * width],
-                    lhsT=weights["w2", e][:, 2 * m * P : 2 * (m + 1) * P].bitcast(FP4),
-                    lhsT_scale=w2s[:, e * N + m * P : e * N + (m + 1) * P],
-                    rhs=hc[:, lo * BLK : lo * BLK + width].bitcast(FP8),
-                    rhs_scale=hs[:, lo * BLK : lo * BLK + width],
-                    start=True,
-                    stop=True,
-                )
-            if b0 == 0:
-                ys = shared[:, 2 * C : 3 * C]
-            else:
-                ys = keep.tile([P, len(halves) * width], F32, name=f"ys{b0}", align_bytes=256, tag=tag or f"ys{b0}")[:]
-            gates = gate_sb[b0 * BLK // half][:, b0 * BLK % half : b0 * BLK % half + width]
-            if not gate_now:
-                nc.scalar.copy(ys[:], sums[:, 0 : len(halves) * width])
-            for i, m in enumerate(halves):
-                part = slice(i * width, (i + 1) * width)
-                if gate_now:
-                    nc.vector.tensor_tensor(ys[:, part], sums[:, part], gates, MULT)
-                y_sb[b0, m] = (ys[:, part], None if gate_now else gates, n)
+        h_codes = [sbuf(f"h_codes{e}", C, U32) for e in range(E)]
+        h_scales = [sbuf(f"h_scales{e}", C, U8) for e in range(E)]
 
-        def place(b0, m):
-            values, gates, n = y_sb[b0, m]
-            window = win[m][:].indirect(dst_sb[:, b0 * BLK // LIST : (b0 + n) * BLK // LIST])
-            if gates is None:
-                nc.vector.tensor_copy(window, values)
-            else:
-                nc.vector.tensor_tensor(window, values, gates, MULT)
+        def quantise_h(s, n):
+            e, lo = divmod(s * SLAB, C)
+            slots = slice(lo, lo + n * SLAB)
+            nc.vector.quantize_mx(out=h_codes[e][:, slots].bitcast(FP8), scales=h_scales[e][:, slots], in_=h_turned[s])
 
-        gather_group(0, 1)
-        gather_group(1, 1)
-        for i in range(GROUPS[LAST_GROUP][1]):
-            gather(LAST_GROUP, 0, i, i + 1)
+        def down(e, m, bank_index, side=0):
+            y_sums[e, m] = bank[bank_index][:, side * C : (side + 1) * C]
+            nc.tensor.matmul_mx(
+                out=y_sums[e, m],
+                lhsT=weights["w2", e][:, WORD * m * P : WORD * (m + 1) * P].bitcast(FP4),
+                lhsT_scale=w2_plane[:, e * N + m * P : e * N + (m + 1) * P],
+                rhs=h_codes[e].bitcast(FP8),
+                rhs_scale=h_scales[e],
+                start=True,
+                stop=True,
+            )
+
+        def gates(e):
+            return gate_sb[e * C // half_slots][:, e * C % half_slots : e * C % half_slots + C]
+
+        def places(e, m):
+            return window[m].indirect(dst_sb[:, e * C // LIST : (e + 1) * C // LIST])
+
+        def gate_out(e, m):
+            y_rows[e, m] = sbuf(f"y{e}{m}", C, F32)
+            nc.vector.tensor_tensor(y_rows[e, m], y_sums[e, m], gates(e), MULT)
+
+        def copy_out(e, m, takes_over=None):
+            y_rows[e, m] = sbuf(f"y{e}{m}", C, F32, takes_over)
+            nc.scalar.copy(y_rows[e, m], y_sums[e, m])
+
+        def scatter_gated(e, m):
+            nc.vector.tensor_copy(places(e, m), y_rows[e, m])
+
+        def gate_and_scatter(e, m):
+            nc.vector.tensor_tensor(places(e, m), y_rows[e, m], gates(e), MULT)
+
+        cast(0)
         quantise_tokens(0)
-        gather_group(2, 1)
-        project(0)
+        cast(1)
         quantise_tokens(1)
-        gather_group(3, 1)
-        project(1)
-        product(0)
-        turn(0)
+        cast(2)
         quantise_tokens(2)
-        gather_group(4, 1)
+        quantise_tokens(3)
+
+        for s0, n in ((0, 1), (1, 1), (2, 2)):
+            gather_codes(s0, n)
+            gather_scales(s0, n)
+        gather_codes(4, 2)
+        project(0)
+        project(1)
+        for s in range(2):
+            product(s)
+            turn(s)
+            collect(s, 1)
+        gather_scales(4, 2, "x_scales1")
+
         project(2)
-        product(1)
-        turn(1)
-        quantise_h(0)
         project(3)
         product(2)
-        quantise_tokens(3)
-        quantise_h(1)
-        product(3)
-        quantise_tokens(4)
-        both = (0, 1)
-        down(0, 0, 1, both, bank[7], False)
-        project(4)
+        quantise_h(0, 1)
+        quantise_h(1, 1)
+        gather_codes(6, 2, "turned0")
+        product(3, "turned1")
         turn(2)
-        product(4)
-        project(5)
-        place(0, 0)
-        place(0, 1)
-        quantise_h(2)
-        product(5)
-        down(1, 0, 1, both, bank[0], True)
-        project(6)
-        product(6)
-        project(7)
-        product(7)
-        place(1, 0)
-        place(1, 1)
-        down(2, 0, 1, both, bank[0], True)
-        turn(3)
-        place(2, 0)
-        place(2, 1)
-        quantise_h(3)
-        down(2, 1, 1, both, bank[0], False, "h4")
-        turn(4)
-        down(3, 0, 2, both, bank[0], False, "h7")
-        place(3, 0)
-        place(3, 1)
-        quantise_h(4)
-        down(4, 0, 2, both, bank[1], False)
-        place(4, 0)
-        place(4, 1)
-        place(6, 0)
-        place(6, 1)
+        gather_scales(6, 2, "h2")
         for m in range(2):
-            nc.sync.dma_start(out=out[m * P : (m + 1) * P, :], in_=win[m][:])
+            down(0, m, FIRST_Y_BANK, m)
+        for m in range(2):
+            gate_out(0, m)
+        project(4)
+        product(4)
+        turn(3)
+        collect(2, 1)
+        collect(3, 1)
+        project(5)
+
+        window[0] = sbuf("window0", T, F32)
+        scatter_gated(0, 0)
+        quantise_h(2, 1)
+        quantise_h(3, 1)
+        product(5, "turned3")
+        window[1] = sbuf("window1", T, F32, "turned2")
+        scatter_gated(0, 1)
+
+        project(6)
+        project(7)
+        down(1, 0, FIRST_Y_BANK)
+        down(1, 1, TURN_BANK[1])
+        gate_out(1, 0)
+        turn(4)
+        turn(5)
+        collect(4, 2)
+        copy_out(1, 1, "turned3")
+        product(6)
+        product(7)
+        scatter_gated(1, 0)
+        quantise_h(4, 2)
+        turn(6)
+        turn(7)
+        collect(6, 2)
+        gate_and_scatter(1, 1)
+
+        quantise_h(6, 2)
+        for e in range(2, E):
+            for m in range(2):
+                down(e, m, LAST_Y_BANKS[2 * (e - 2) + m])
+                copy_out(e, m, "h7" if (e, m) == (2, 0) else None)
+                gate_and_scatter(e, m)
+        for m in range(2):
+            nc.sync.dma_start(out=out[m * P : (m + 1) * P, :], in_=window[m])

@@ -12,16 +12,15 @@ LIST = 16
 WORD = 2
 NEIGHBOURS = 4
 
-CHUNKS = ((0, 512, 320), (512, 320, 128), (832, 192, 128))
-RUN = 256
+CHUNKS = (((0, 768, 480), (768, 256, 160)), ((0, 256, 0), (256, 256, 0), (512, 256, 0), (768, 256, 0)))
 
-FIRST_ON_GPSIMD = 3
+STAGE_BLOCK = (1, 4, 0, 3)
 
-A_BANK = (2, 3, 2, 3, 2, 3, 2, 3)
-B_BANK = (4, 5, 6, 5, 4, 6, 5, 4)
-TURN_BANK = (0, 1, 0, 0, 6, 6, 0, 0)
-FIRST_Y_BANK = 7
-LAST_Y_BANKS = (2, 3, 4, 5)
+A_BANK = (0, 1, 6, 7, 0, 1, 0, 1)
+B_BANK = (2, 3, 4, 2, 3, 4, 2, 3)
+TURN_BANK = (5, 6, 5, 6)
+Y_BANK = (7, 0, 2, 1)
+Y_HALF = ((7, 0), (4, 1), (2, 5), (3, 6))
 
 F32 = mybir.dt.float32
 BF16 = mybir.dt.bfloat16
@@ -51,15 +50,14 @@ def tile_moe_two_glu_silu_kernel(
         w1_plane = sbuf("w1_plane", E * H, U8)
         w3_plane = sbuf("w3_plane", E * H, U8)
         w2_plane = sbuf("w2_plane", E * N, U8)
-        rounded = sbuf("rounded", 4 * T, BF16)
-        token_codes = sbuf("token_codes", T, U32)
-        token_plane = sbuf("token_plane", T, U8)
+        pairs = [sbuf(f"pairs{u}", 2 * T, BF16) for u in range(2)]
+        stage = sbuf("stage", (E + 2) * C, U32)
         ident = sbuf("ident", P, F32)
         half_slots = E * C // 2
         gate_sb = [sbuf(f"gate{i}", half_slots, F32) for i in range(2)]
         bank = [psum.tile([P, 4 * SLAB], F32, name=f"bank{i}") for i in range(8)]
 
-        for plane in (w1_plane, w3_plane, w2_plane, token_plane):
+        for plane in (w1_plane, w3_plane, w2_plane):
             nc.vector.memset(plane.bitcast(I32), 0)
         table_warm = keep.tile([P, 1], F32, name="table_warm")
         nc.vector.memset(table_warm[:], 0.0)
@@ -72,12 +70,13 @@ def tile_moe_two_glu_silu_kernel(
                 )
 
         x_rows = xT.rearrange("(p j) t -> p j t", j=4)
-        raw = []
-        for i, (t0, width, by_vector) in enumerate(CHUNKS):
-            chunk = keep.tile([P, 4, width], F32, name=f"raw{i}", align_bytes=256)[:]
-            nc.sync.dma_start(out=chunk, in_=x_rows[:, :, t0 : t0 + width])
-            raw.append(chunk)
-        nc.sync.dma_start(offs_sb[:], offs)
+        raw = {}
+        for u in range(2):
+            for i, (t0, width, by_vector) in enumerate(CHUNKS[u]):
+                raw[u, i] = keep.tile([P, 2, width], F32, name=f"raw{u}{i}", align_bytes=256)[:]
+                nc.sync.dma_start(out=raw[u, i], in_=x_rows[:, 2 * u : 2 * u + 2, t0 : t0 + width])
+                if (u, i) == (0, 0):
+                    nc.sync.dma_start(offs_sb[:], offs)
         nc.scalar.activation(table_warm[:], table_warm[:], ACT.Silu)
         make_identity(nc, ident)
 
@@ -89,48 +88,56 @@ def tile_moe_two_glu_silu_kernel(
             for i in range(n):
                 weights[key, e0 + i] = rows[:, i, :]
 
-        load_words("w1", w1_words, 0, 1)
+        load_words("w1", w1_words, 0, 2)
         load_scales(w1_plane, w1_scales)
         load_scales(w2_plane, w2_scales)
-        load_words("w3", w3_words, 0, 1)
+        load_words("w3", w3_words, 0, 2)
         load_scales(w3_plane, w3_scales)
-        for e0, n in ((1, 1), (2, E - 2)):
-            load_words("w1", w1_words, e0, n)
-            load_words("w3", w3_words, e0, n)
+        load_words("w1", w1_words, 2, 2)
+        load_words("w3", w3_words, 2, 2)
         load_words("w2", w2_words, 0, E)
         nc.sync.dma_start(out=gate_sb[0], in_=gate[0:P, 0:half_slots])
         nc.sync.dma_start(dst_sb[:], dst)
         nc.sync.dma_start(out=gate_sb[1], in_=gate[0:P, half_slots:])
 
-        def cast(i):
-            t0, width, by_vector = CHUNKS[i]
+        def cast(u, i):
+            t0, width, by_vector = CHUNKS[u][i]
             for lo, hi, copy in ((0, by_vector, nc.vector.tensor_copy), (by_vector, width, nc.scalar.copy)):
-                values = rounded[:, 4 * (t0 + lo) : 4 * (t0 + hi)].rearrange("p (c t j) -> p c j t", t=NEIGHBOURS, j=4)
-                copy(values, raw[i][:, :, lo:hi].rearrange("p j (c t) -> p c j t", t=NEIGHBOURS))
+                if lo < hi:
+                    values = pairs[u][:, 2 * (t0 + lo) : 2 * (t0 + hi)].rearrange("p (c t j) -> p c j t", t=NEIGHBOURS, j=2)
+                    copy(values, raw[u, i][:, :, lo:hi].rearrange("p j (c t) -> p c j t", t=NEIGHBOURS))
 
-        def quantise_tokens(r):
-            tokens = slice(r * RUN, (r + 1) * RUN)
-            nc.vector.quantize_mx(
-                out=token_codes[:, tokens].bitcast(FP8),
-                scales=token_plane[:, tokens],
-                in_=rounded[:, 4 * r * RUN : 4 * (r + 1) * RUN],
-            )
+        def staged(s, n):
+            e, lo = divmod(s * SLAB, C)
+            both = stage[:, STAGE_BLOCK[e] * C : (STAGE_BLOCK[e] + 2) * C].rearrange("p (u s) -> p u s", u=2)
+            return both[:, :, lo : lo + n * SLAB]
 
-        x_codes, x_scales = {}, {}
+        def gather(u, s, n):
+            offsets = offs_sb[:, s * SLAB // LIST : (s + n) * SLAB // LIST]
+            nc.vector.tensor_copy(staged(s, n)[:, u, :], pairs[u].bitcast(U32).indirect(offsets))
 
-        def gather(name, dtype, window, found, s0, n, takes_over):
-            picked = sbuf(f"{name}{s0}", n * SLAB, dtype, takes_over)
-            nc.vector.tensor_copy(picked, window.indirect(offs_sb[:, s0 * SLAB // LIST : (s0 + n) * SLAB // LIST]))
+        woven, x_codes, x_scales = {}, {}, {}
+
+        def weave(s, n, on_vector=False, takes_over=None):
+            woven[s] = sbuf(f"woven{s}", 4 * n * SLAB, BF16, takes_over)
+            words = woven[s].bitcast(U32).rearrange("p (s u) -> p s u", u=2)
+            source = staged(s, n).rearrange("p u s -> p s u")
+            if on_vector:
+                nc.vector.tensor_copy(woven[s].bitcast(I32).rearrange("p (s u) -> p s u", u=2), staged_i32(s, n))
+            else:
+                nc.scalar.copy(words, source)
+
+        def staged_i32(s, n):
+            return staged(s, n).bitcast(I32).rearrange("p u s -> p s u")
+
+        def quantise_x(s, n, takes_over=None):
+            codes, scales = sbuf(f"x_codes{s}", n * SLAB, U32, takes_over), sbuf(f"x_scales{s}", n * SLAB, U8)
+            nc.vector.quantize_mx(out=codes.bitcast(FP8), scales=scales, in_=woven[s])
             for i in range(n):
-                found[s0 + i] = picked[:, i * SLAB : (i + 1) * SLAB]
+                x_codes[s + i] = codes[:, i * SLAB : (i + 1) * SLAB]
+                x_scales[s + i] = scales[:, i * SLAB : (i + 1) * SLAB]
 
-        def gather_codes(s0, n, takes_over=None):
-            gather("x_codes", U32, token_codes, x_codes, s0, n, takes_over)
-
-        def gather_scales(s0, n, takes_over=None):
-            gather("x_scales", U8, token_plane, x_scales, s0, n, takes_over)
-
-        silu_a, sums_b, h_rows, h_turned, y_sums, y_rows, window = {}, {}, {}, {}, {}, {}, {}
+        silu_a, sums_b, h_rows, h_turned, y_rows, window = {}, {}, {}, {}, {}, {}
 
         def by_pair(sums):
             return sums[:].rearrange("s (q u d) -> s u q d", u=2, d=2)
@@ -138,160 +145,184 @@ def tile_moe_two_glu_silu_kernel(
         def in_pair_order(tile):
             return tile.rearrange("s (u q d) -> s u q d", u=2, d=2)
 
-        def project(s):
+        def first_layer(s, sums, key, plane):
             e = s * SLAB // C
-            pa, pb = bank[A_BANK[s]], bank[B_BANK[s]]
-            for sums, key, plane in ((pa, "w1", w1_plane), (pb, "w3", w3_plane)):
-                nc.tensor.matmul_mx(
-                    out=sums[:],
-                    lhsT=x_codes[s].bitcast(FP8),
-                    lhsT_scale=x_scales[s],
-                    rhs=weights[key, e].bitcast(FP4),
-                    rhs_scale=plane[:, e * H : (e + 1) * H],
-                    start=True,
-                    stop=True,
-                )
+            nc.tensor.matmul_mx(
+                out=sums[:],
+                lhsT=x_codes[s].bitcast(FP8),
+                lhsT_scale=x_scales[s],
+                rhs=weights[key, e].bitcast(FP4),
+                rhs_scale=plane[:, e * H : (e + 1) * H],
+                start=True,
+                stop=True,
+            )
+
+        def pass_a(s):
+            first_layer(s, bank[A_BANK[s]], "w1", w1_plane)
             silu_a[s] = sbuf(f"silu{s}", H, F32)
-            nc.scalar.activation(in_pair_order(silu_a[s]), by_pair(pa), ACT.Silu)
-            if s < FIRST_ON_GPSIMD:
-                sums_b[s] = by_pair(pb)
-            else:
-                sums_b[s] = sbuf(f"b{s}", H, F32)
-                nc.scalar.copy(in_pair_order(sums_b[s]), by_pair(pb))
+            nc.scalar.activation(in_pair_order(silu_a[s]), by_pair(bank[A_BANK[s]]), ACT.Silu)
+
+        def pass_b(s):
+            first_layer(s, bank[B_BANK[s]], "w3", w3_plane)
 
         def product(s, takes_over=None):
             h_rows[s] = sbuf(f"h{s}", H, BF16, takes_over)
-            if s < FIRST_ON_GPSIMD:
-                nc.vector.tensor_tensor(in_pair_order(h_rows[s]), in_pair_order(silu_a[s]), sums_b[s], MULT)
-            else:
-                nc.gpsimd.tensor_tensor(h_rows[s], silu_a[s], sums_b[s], MULT)
-
-        def turn_columns(s, n):
-            side = s % 2 if s > 1 else 0
-            columns = bank[TURN_BANK[s]][:, 2 * side * SLAB : 2 * (side + n) * SLAB]
-            return columns.rearrange("p (b u s) -> p b u s", b=n, u=2)
+            nc.vector.tensor_tensor(in_pair_order(h_rows[s]), in_pair_order(silu_a[s]), by_pair(bank[B_BANK[s]]), MULT)
 
         def turn(s):
+            columns = bank[TURN_BANK[s // 2]][:].rearrange("p (b u s) -> p b u s", b=2, u=2)
             h_words = h_rows[s].bitcast(F32)
             for u in range(2):
-                nc.tensor.transpose(turn_columns(s, 1)[:, 0, u, :], h_words[:, u * P : (u + 1) * P], ident)
+                nc.tensor.transpose(columns[:, s % 2, u, :], h_words[:, u * P : (u + 1) * P], ident)
 
-        def collect(s, n):
-            h_turned[s] = sbuf(f"turned{s}", n * SLAB * 4, BF16)
-            words = h_turned[s].bitcast(F32).rearrange("p (b s u) -> p b s u", b=n, u=2)
-            nc.scalar.copy(words, turn_columns(s, n).rearrange("p b u s -> p b s u"))
+        def collect(e, takes_over=None, copy=nc.scalar.copy):
+            h_turned[e] = sbuf(f"turned{e}", C * 4, BF16, takes_over)
+            words = h_turned[e].bitcast(F32).rearrange("p (b s u) -> p b s u", b=2, u=2)
+            copy(words, bank[TURN_BANK[e]][:].rearrange("p (b u s) -> p b s u", b=2, u=2))
 
-        h_codes = [sbuf(f"h_codes{e}", C, U32) for e in range(E)]
-        h_scales = [sbuf(f"h_scales{e}", C, U8) for e in range(E)]
+        h_codes = {}
 
-        def quantise_h(s, n):
-            e, lo = divmod(s * SLAB, C)
-            slots = slice(lo, lo + n * SLAB)
-            nc.vector.quantize_mx(out=h_codes[e][:, slots].bitcast(FP8), scales=h_scales[e][:, slots], in_=h_turned[s])
+        def quantise_h(e):
+            h_codes[e] = sbuf(f"h_codes{e}", C, U32), sbuf(f"h_scales{e}", C, U8)
+            nc.vector.quantize_mx(out=h_codes[e][0].bitcast(FP8), scales=h_codes[e][1], in_=h_turned[e])
 
-        def down(e, m, bank_index, side=0):
-            y_sums[e, m] = bank[bank_index][:, side * C : (side + 1) * C]
-            nc.tensor.matmul_mx(
-                out=y_sums[e, m],
-                lhsT=weights["w2", e][:, WORD * m * P : WORD * (m + 1) * P].bitcast(FP4),
-                lhsT_scale=w2_plane[:, e * N + m * P : e * N + (m + 1) * P],
-                rhs=h_codes[e].bitcast(FP8),
-                rhs_scale=h_scales[e],
-                start=True,
-                stop=True,
+        def down(e):
+            codes, scales = h_codes[e]
+            for m in (1, 0):
+                nc.tensor.matmul_mx(
+                    out=bank[Y_HALF[e][m]][:, m * C : (m + 1) * C],
+                    lhsT=weights["w2", e][:, WORD * m * P : WORD * (m + 1) * P].bitcast(FP4),
+                    lhsT_scale=w2_plane[:, e * N + m * P : e * N + (m + 1) * P],
+                    rhs=codes.bitcast(FP8),
+                    rhs_scale=scales,
+                    start=True,
+                    stop=True,
+                )
+
+        def gate_out(e, takes_over=None):
+            y_rows[e] = sbuf(f"y{e}", 2 * C, F32, takes_over)
+            gates = gate_sb[e * C // half_slots][:, e * C % half_slots : e * C % half_slots + C]
+            nc.vector.tensor_tensor(
+                y_rows[e].rearrange("p (m s) -> p m s", m=2),
+                bank[Y_BANK[e]][:].rearrange("p (m s) -> p m s", m=2),
+                gates.unsqueeze(1).to_broadcast([P, 2, C]),
+                MULT,
             )
 
         def gates(e):
             return gate_sb[e * C // half_slots][:, e * C % half_slots : e * C % half_slots + C]
 
+        def y_tiles(e, takes_over):
+            both = sbuf(f"y{e}", 2 * C, F32, takes_over)
+            for m in range(2):
+                y_rows[e, m] = both[:, m * C : (m + 1) * C]
+
+        def gate_half(e, m, takes_over=None):
+            if (e, m) not in y_rows:
+                y_rows[e, m] = sbuf(f"y{e}{m}", C, F32, takes_over)
+            nc.vector.tensor_tensor(y_rows[e, m], bank[Y_HALF[e][m]][:, m * C : (m + 1) * C], gates(e), MULT)
+
+        def copy_half(e, m, takes_over=None):
+            if (e, m) not in y_rows:
+                y_rows[e, m] = sbuf(f"y{e}{m}", C, F32, takes_over)
+            nc.scalar.copy(y_rows[e, m], bank[Y_HALF[e][m]][:, m * C : (m + 1) * C])
+
         def places(e, m):
             return window[m].indirect(dst_sb[:, e * C // LIST : (e + 1) * C // LIST])
 
-        def gate_out(e, m):
-            y_rows[e, m] = sbuf(f"y{e}{m}", C, F32)
-            nc.vector.tensor_tensor(y_rows[e, m], y_sums[e, m], gates(e), MULT)
-
-        def copy_out(e, m, takes_over=None):
-            y_rows[e, m] = sbuf(f"y{e}{m}", C, F32, takes_over)
-            nc.scalar.copy(y_rows[e, m], y_sums[e, m])
-
-        def scatter_gated(e, m):
-            nc.vector.tensor_copy(places(e, m), y_rows[e, m])
+        def scatter_half(e, m):
+            nc.scalar.activation(places(e, m), y_rows[e, m], ACT.Copy)
 
         def gate_and_scatter(e, m):
             nc.vector.tensor_tensor(places(e, m), y_rows[e, m], gates(e), MULT)
 
-        cast(0)
-        quantise_tokens(0)
-        cast(1)
-        quantise_tokens(1)
-        cast(2)
-        quantise_tokens(2)
-        quantise_tokens(3)
+        def scatter(e, m, on_vector, lo=0, hi=C):
+            places = window[m].indirect(dst_sb[:, (e * C + lo) // LIST : (e * C + hi) // LIST])
+            values = y_rows[e][:, m * C + lo : m * C + hi]
+            if on_vector:
+                nc.vector.tensor_copy(places, values)
+            else:
+                nc.scalar.activation(places, values, ACT.Copy)
 
-        for s0, n in ((0, 1), (1, 1), (2, 2)):
-            gather_codes(s0, n)
-            gather_scales(s0, n)
-        gather_codes(4, 2)
-        project(0)
-        project(1)
-        for s in range(2):
-            product(s)
-            turn(s)
-            collect(s, 1)
-        gather_scales(4, 2, "x_scales1")
-
-        project(2)
-        project(3)
+        for i in range(len(CHUNKS[0])):
+            cast(0, i)
+        for e in range(E):
+            gather(0, 2 * e, 2)
+        for i in range(len(CHUNKS[1])):
+            cast(1, i)
+        for s, n in ((0, 1), (1, 1), (2, 2)):
+            gather(1, s, n)
+            weave(s, n)
+        quantise_x(0, 1)
+        quantise_x(1, 1)
+        gather(1, 4, 2)
+        quantise_x(2, 2)
+        gather(1, 6, 2)
+        weave(4, 2)
+        quantise_x(4, 2)
+        weave(6, 2, True)
+        pass_a(0)
+        pass_a(1)
+        pass_b(0)
+        pass_b(1)
+        pass_a(2)
+        pass_a(3)
+        product(0)
+        pass_b(2)
+        product(1)
+        quantise_x(6, 2, "x_codes0")
+        pass_a(4)
+        pass_a(5)
+        turn(0)
+        turn(1)
+        collect(0)
+        pass_b(3)
         product(2)
-        quantise_h(0, 1)
-        quantise_h(1, 1)
-        gather_codes(6, 2, "turned0")
-        product(3, "turned1")
+        pass_b(4)
+        product(3)
+        quantise_h(0)
+        pass_a(6)
+        pass_a(7)
+        pass_b(5)
+        pass_b(6)
         turn(2)
-        gather_scales(6, 2, "h2")
-        for m in range(2):
-            down(0, m, FIRST_Y_BANK, m)
-        for m in range(2):
-            gate_out(0, m)
-        project(4)
-        product(4)
         turn(3)
-        collect(2, 1)
-        collect(3, 1)
-        project(5)
-
-        window[0] = sbuf("window0", T, F32)
-        scatter_gated(0, 0)
-        quantise_h(2, 1)
-        quantise_h(3, 1)
-        product(5, "turned3")
-        window[1] = sbuf("window1", T, F32, "turned2")
-        scatter_gated(0, 1)
-
-        project(6)
-        project(7)
-        down(1, 0, FIRST_Y_BANK)
-        down(1, 1, TURN_BANK[1])
-        gate_out(1, 0)
-        turn(4)
-        turn(5)
-        collect(4, 2)
-        copy_out(1, 1, "turned3")
+        collect(1)
+        product(4)
+        pass_b(7)
+        down(0)
+        product(5)
         product(6)
         product(7)
-        scatter_gated(1, 0)
-        quantise_h(4, 2)
+        copy_half(0, 0)
+        gate_half(0, 1)
+        quantise_h(1)
+        turn(4)
+        turn(5)
+        collect(2)
         turn(6)
         turn(7)
-        collect(6, 2)
-        gate_and_scatter(1, 1)
-
-        quantise_h(6, 2)
-        for e in range(2, E):
-            for m in range(2):
-                down(e, m, LAST_Y_BANKS[2 * (e - 2) + m])
-                copy_out(e, m, "h7" if (e, m) == (2, 0) else None)
-                gate_and_scatter(e, m)
-        for m in range(2):
+        collect(3)
+        down(1)
+        window[0] = sbuf("window0", T, F32)
+        window[1] = sbuf("window1", T, F32, "h7")
+        scatter_half(0, 1)
+        gate_and_scatter(0, 0)
+        quantise_h(2)
+        quantise_h(3)
+        down(2)
+        down(3)
+        gate_half(1, 1)
+        copy_half(1, 0)
+        gate_half(2, 1)
+        gate_and_scatter(1, 0)
+        scatter_half(1, 1)
+        gate_half(3, 1)
+        copy_half(2, 0)
+        gate_and_scatter(2, 0)
+        scatter_half(2, 1)
+        copy_half(3, 0)
+        gate_and_scatter(3, 0)
+        scatter_half(3, 1)
+        for m in (1, 0):
             nc.sync.dma_start(out=out[m * P : (m + 1) * P, :], in_=window[m])

@@ -119,7 +119,10 @@ def tile_moe_two_glu_silu_kernel(
         woven, x_codes, x_scales = {}, {}, {}
 
         def weave(s, n, on_vector=False, takes_over=None):
-            woven[s] = sbuf(f"woven{s}", 4 * n * SLAB, BF16, takes_over)
+            if s == 6:
+                woven[s] = stage[:, 0 : 2 * C].bitcast(BF16)
+            else:
+                woven[s] = sbuf(f"woven{s}", 4 * n * SLAB, BF16, takes_over)
             words = woven[s].bitcast(U32).rearrange("p (s u) -> p s u", u=2)
             source = staged(s, n).rearrange("p u s -> p s u")
             if on_vector:
@@ -273,10 +276,10 @@ def tile_moe_two_glu_silu_kernel(
         quantise_x(6, 2, "x_codes0")
         pass_a(4)
         pass_a(5)
+        pass_b(3)
         turn(0)
         turn(1)
         collect(0)
-        pass_b(3)
         product(2)
         pass_b(4)
         product(3)
@@ -290,39 +293,39 @@ def tile_moe_two_glu_silu_kernel(
         collect(1)
         product(4)
         pass_b(7)
-        down(0)
         product(5)
-        product(6)
-        product(7)
-        copy_half(0, 0)
-        gate_half(0, 1)
-        quantise_h(1)
         turn(4)
         turn(5)
         collect(2)
+        down(0)
+        product(6)
+        product(7)
+        quantise_h(1)
+        copy_half(0, 0)
+        gate_half(0, 1)
+        quantise_h(2)
         turn(6)
         turn(7)
-        collect(3)
         down(1)
-        window[0] = sbuf("window0", T, F32)
+        collect(3)
+        window[0] = sbuf("window0", T, F32, "h5")
         window[1] = sbuf("window1", T, F32, "h7")
         scatter_half(0, 1)
-        gate_and_scatter(0, 0)
-        quantise_h(2)
-        quantise_h(3)
         down(2)
-        down(3)
+        gate_and_scatter(0, 0)
         gate_half(1, 1)
+        quantise_h(3)
+        down(3)
         copy_half(1, 0)
+        scatter_half(1, 1)
         gate_half(2, 1)
         gate_and_scatter(1, 0)
-        scatter_half(1, 1)
-        gate_half(3, 1)
-        copy_half(2, 0)
-        gate_and_scatter(2, 0)
+        copy_half(2, 0, "turned3")
         scatter_half(2, 1)
+        gate_half(3, 1)
+        gate_and_scatter(2, 0)
         copy_half(3, 0)
-        gate_and_scatter(3, 0)
         scatter_half(3, 1)
+        gate_and_scatter(3, 0)
         for m in (1, 0):
             nc.sync.dma_start(out=out[m * P : (m + 1) * P, :], in_=window[m])

@@ -12,14 +12,13 @@ LIST = 16
 WORD = 2
 NEIGHBOURS = 4
 
-CHUNKS = (((0, 768, 480), (768, 256, 160)), ((0, 256, 0), (256, 256, 0), (512, 256, 0), (768, 256, 0)))
+CHUNKS = (((0, 768, 480, 0), (768, 256, 160, 0)), ((0, 320, 0, 96), (320, 320, 0, 96), (640, 256, 0, 80), (896, 128, 0, 32)))
 
-STAGE_BLOCK = (1, 4, 0, 3)
+STAGE_BLOCK = (2, 3, 0, 1)
 
 A_BANK = (0, 1, 6, 7, 0, 1, 0, 1)
 B_BANK = (2, 3, 4, 2, 3, 4, 2, 3)
 TURN_BANK = (5, 6, 5, 6)
-Y_BANK = (7, 0, 2, 1)
 Y_HALF = ((7, 0), (4, 1), (2, 5), (3, 6))
 
 F32 = mybir.dt.float32
@@ -57,10 +56,10 @@ def tile_moe_two_glu_silu_kernel(
         gate_sb = [sbuf(f"gate{i}", half_slots, F32) for i in range(2)]
         bank = [psum.tile([P, 4 * SLAB], F32, name=f"bank{i}") for i in range(8)]
 
-        for plane in (w1_plane, w3_plane, w2_plane):
-            nc.vector.memset(plane.bitcast(I32), 0)
         table_warm = keep.tile([P, 1], F32, name="table_warm")
         nc.vector.memset(table_warm[:], 0.0)
+        for plane in (w1_plane, w3_plane, w2_plane):
+            nc.vector.memset(plane.bitcast(I32), 0)
 
         def load_scales(plane, src):
             for q in (0, 2, 1, 3):
@@ -72,10 +71,10 @@ def tile_moe_two_glu_silu_kernel(
         x_rows = xT.rearrange("(p j) t -> p j t", j=4)
         raw = {}
         for u in range(2):
-            for i, (t0, width, by_vector) in enumerate(CHUNKS[u]):
+            for i, (t0, width, by_vector, by_gpsimd) in enumerate(CHUNKS[u]):
                 raw[u, i] = keep.tile([P, 2, width], F32, name=f"raw{u}{i}", align_bytes=256)[:]
                 nc.sync.dma_start(out=raw[u, i], in_=x_rows[:, 2 * u : 2 * u + 2, t0 : t0 + width])
-                if (u, i) == (0, 0):
+                if (u, i) == (0, 1):
                     nc.sync.dma_start(offs_sb[:], offs)
         nc.scalar.activation(table_warm[:], table_warm[:], ACT.Silu)
         make_identity(nc, ident)
@@ -101,26 +100,30 @@ def tile_moe_two_glu_silu_kernel(
         nc.sync.dma_start(out=gate_sb[1], in_=gate[0:P, half_slots:])
 
         def cast(u, i):
-            t0, width, by_vector = CHUNKS[u][i]
-            for lo, hi, copy in ((0, by_vector, nc.vector.tensor_copy), (by_vector, width, nc.scalar.copy)):
+            t0, width, by_vector, by_gpsimd = CHUNKS[u][i]
+            for lo, hi, copy in ((0, by_vector, nc.vector.tensor_copy), (by_vector, width - by_gpsimd, nc.scalar.copy)):
                 if lo < hi:
                     values = pairs[u][:, 2 * (t0 + lo) : 2 * (t0 + hi)].rearrange("p (c t j) -> p c j t", t=NEIGHBOURS, j=2)
                     copy(values, raw[u, i][:, :, lo:hi].rearrange("p j (c t) -> p c j t", t=NEIGHBOURS))
+            if by_gpsimd:
+                values = pairs[u][:, 2 * (t0 + width - by_gpsimd) : 2 * (t0 + width)].rearrange("p (t j) -> p t j", j=2)
+                nc.gpsimd.tensor_copy(values, raw[u, i][:, :, width - by_gpsimd : width].rearrange("p j t -> p t j"))
 
         def staged(s, n):
             e, lo = divmod(s * SLAB, C)
-            both = stage[:, STAGE_BLOCK[e] * C : (STAGE_BLOCK[e] + 2) * C].rearrange("p (u s) -> p u s", u=2)
+            both = stage.rearrange("p (b s) -> p b s", s=C)[:, STAGE_BLOCK[e] : STAGE_BLOCK[e] + 3 : 2, :]
             return both[:, :, lo : lo + n * SLAB]
 
         def gather(u, s, n):
             offsets = offs_sb[:, s * SLAB // LIST : (s + n) * SLAB // LIST]
-            nc.vector.tensor_copy(staged(s, n)[:, u, :], pairs[u].bitcast(U32).indirect(offsets))
+            first = (STAGE_BLOCK[s * SLAB // C] + 2 * u) * C + s * SLAB % C
+            nc.vector.tensor_copy(stage[:, first : first + n * SLAB], pairs[u].bitcast(U32).indirect(offsets))
 
         woven, x_codes, x_scales = {}, {}, {}
 
         def weave(s, n, on_vector=False, takes_over=None):
             if s == 6:
-                woven[s] = stage[:, 0 : 2 * C].bitcast(BF16)
+                woven[s] = sbuf("woven6", 4 * n * SLAB, BF16, "woven2")
             else:
                 woven[s] = sbuf(f"woven{s}", 4 * n * SLAB, BF16, takes_over)
             words = woven[s].bitcast(U32).rearrange("p (s u) -> p s u", u=2)
@@ -202,55 +205,33 @@ def tile_moe_two_glu_silu_kernel(
                     stop=True,
                 )
 
-        def gate_out(e, takes_over=None):
-            y_rows[e] = sbuf(f"y{e}", 2 * C, F32, takes_over)
-            gates = gate_sb[e * C // half_slots][:, e * C % half_slots : e * C % half_slots + C]
-            nc.vector.tensor_tensor(
-                y_rows[e].rearrange("p (m s) -> p m s", m=2),
-                bank[Y_BANK[e]][:].rearrange("p (m s) -> p m s", m=2),
-                gates.unsqueeze(1).to_broadcast([P, 2, C]),
-                MULT,
-            )
-
         def gates(e):
             return gate_sb[e * C // half_slots][:, e * C % half_slots : e * C % half_slots + C]
 
-        def y_tiles(e, takes_over):
-            both = sbuf(f"y{e}", 2 * C, F32, takes_over)
-            for m in range(2):
-                y_rows[e, m] = both[:, m * C : (m + 1) * C]
+        def sums(e, m, lo, hi):
+            return bank[Y_HALF[e][m]][:, m * C + lo : m * C + hi]
 
-        def gate_half(e, m, takes_over=None):
-            if (e, m) not in y_rows:
-                y_rows[e, m] = sbuf(f"y{e}{m}", C, F32, takes_over)
-            nc.vector.tensor_tensor(y_rows[e, m], bank[Y_HALF[e][m]][:, m * C : (m + 1) * C], gates(e), MULT)
+        def gate_half(e, m, takes_over=None, lo=0, hi=C):
+            y_rows[e, m, lo] = sbuf(f"y{e}{m}_{lo}", hi - lo, F32, takes_over)
+            nc.vector.tensor_tensor(y_rows[e, m, lo], sums(e, m, lo, hi), gates(e)[:, lo:hi], MULT)
 
-        def copy_half(e, m, takes_over=None):
-            if (e, m) not in y_rows:
-                y_rows[e, m] = sbuf(f"y{e}{m}", C, F32, takes_over)
-            nc.scalar.copy(y_rows[e, m], bank[Y_HALF[e][m]][:, m * C : (m + 1) * C])
+        def copy_half(e, m, takes_over=None, lo=0, hi=C):
+            y_rows[e, m, lo] = sbuf(f"y{e}{m}_{lo}", hi - lo, F32, takes_over)
+            nc.scalar.copy(y_rows[e, m, lo], sums(e, m, lo, hi))
 
-        def places(e, m):
-            return window[m].indirect(dst_sb[:, e * C // LIST : (e + 1) * C // LIST])
+        def places(e, m, lo, hi):
+            return window[m].indirect(dst_sb[:, (e * C + lo) // LIST : (e * C + hi) // LIST])
 
-        def scatter_half(e, m):
-            nc.scalar.activation(places(e, m), y_rows[e, m], ACT.Copy)
+        def scatter_half(e, m, lo=0, hi=C):
+            nc.scalar.activation(places(e, m, lo, hi), y_rows[e, m, lo], ACT.Copy)
 
-        def gate_and_scatter(e, m):
-            nc.vector.tensor_tensor(places(e, m), y_rows[e, m], gates(e), MULT)
-
-        def scatter(e, m, on_vector, lo=0, hi=C):
-            places = window[m].indirect(dst_sb[:, (e * C + lo) // LIST : (e * C + hi) // LIST])
-            values = y_rows[e][:, m * C + lo : m * C + hi]
-            if on_vector:
-                nc.vector.tensor_copy(places, values)
-            else:
-                nc.scalar.activation(places, values, ACT.Copy)
+        def gate_and_scatter(e, m, lo=0, hi=C):
+            nc.vector.tensor_tensor(places(e, m, lo, hi), y_rows[e, m, lo], gates(e)[:, lo:hi], MULT)
 
         for i in range(len(CHUNKS[0])):
             cast(0, i)
-        for e in range(E):
-            gather(0, 2 * e, 2)
+        for s in (0, 4):
+            gather(0, s, 4)
         for i in range(len(CHUNKS[1])):
             cast(1, i)
         for s, n in ((0, 1), (1, 1), (2, 2)):

@@ -16,10 +16,10 @@ CHUNKS = (((0, 768, 480, 0), (768, 256, 160, 0)), ((0, 320, 0, 96), (320, 320, 0
 
 STAGE_BLOCK = (2, 3, 0, 1)
 
-A_BANK = (0, 1, 6, 7, 0, 1, 0, 1)
+A_BANK = (0, 1, 6, 7, 0, 1, 6, 7)
 B_BANK = (2, 3, 4, 2, 3, 4, 2, 3)
-TURN_BANK = (5, 6, 5, 6)
-Y_HALF = ((7, 0), (4, 1), (2, 5), (3, 6))
+TURN_BANK = (5, 0, 5, 6)
+Y_HALF = ((1, 4), (0, 7), (2, 5), (3, 1))
 
 F32 = mybir.dt.float32
 BF16 = mybir.dt.bfloat16
@@ -50,7 +50,7 @@ def tile_moe_two_glu_silu_kernel(
         w3_plane = sbuf("w3_plane", E * H, U8)
         w2_plane = sbuf("w2_plane", E * N, U8)
         pairs = [sbuf(f"pairs{u}", 2 * T, BF16) for u in range(2)]
-        stage = sbuf("stage", (E + 2) * C, U32)
+        stage = sbuf("stage", (E + 3) * C, U32)
         ident = sbuf("ident", P, F32)
         half_slots = E * C // 2
         gate_sb = [sbuf(f"gate{i}", half_slots, F32) for i in range(2)]
@@ -61,8 +61,8 @@ def tile_moe_two_glu_silu_kernel(
         for plane in (w1_plane, w3_plane, w2_plane):
             nc.vector.memset(plane.bitcast(I32), 0)
 
-        def load_scales(plane, src):
-            for q in (0, 2, 1, 3):
+        def load_scales(plane, src, quadrants=(0, 2, 1, 3)):
+            for q in quadrants:
                 nc.sync.dma_start(
                     out=plane[32 * q : 32 * q + 4, :].rearrange("r (e i) -> r e i", e=E).bitcast(I32),
                     in_=src[:, 0, 4 * q : 4 * q + 4, :].rearrange("e r i -> r e i").bitcast(I32),
@@ -87,13 +87,15 @@ def tile_moe_two_glu_silu_kernel(
             for i in range(n):
                 weights[key, e0 + i] = rows[:, i, :]
 
+        load_words("w3", w3_words, 0, 1)
+        load_scales(w3_plane, w3_scales, (0, 2, 1))
         load_words("w1", w1_words, 0, 2)
-        load_scales(w1_plane, w1_scales)
-        load_scales(w2_plane, w2_scales)
-        load_words("w3", w3_words, 0, 2)
-        load_scales(w3_plane, w3_scales)
+        load_scales(w1_plane, w1_scales, (2, 0, 3, 1))
+        load_scales(w3_plane, w3_scales, (3,))
+        load_words("w3", w3_words, 1, 1)
         load_words("w1", w1_words, 2, 2)
         load_words("w3", w3_words, 2, 2)
+        load_scales(w2_plane, w2_scales)
         load_words("w2", w2_words, 0, E)
         nc.sync.dma_start(out=gate_sb[0], in_=gate[0:P, 0:half_slots])
         nc.sync.dma_start(dst_sb[:], dst)
@@ -121,20 +123,12 @@ def tile_moe_two_glu_silu_kernel(
 
         woven, x_codes, x_scales = {}, {}, {}
 
-        def weave(s, n, on_vector=False, takes_over=None):
-            if s == 6:
-                woven[s] = sbuf("woven6", 4 * n * SLAB, BF16, "woven2")
+        def weave(s, n, copy=nc.scalar.copy, word=U32, takes_over=None):
+            if s >= 4:
+                woven[s] = stage[:, (E + 1) * C : (E + 3) * C].bitcast(BF16)
             else:
                 woven[s] = sbuf(f"woven{s}", 4 * n * SLAB, BF16, takes_over)
-            words = woven[s].bitcast(U32).rearrange("p (s u) -> p s u", u=2)
-            source = staged(s, n).rearrange("p u s -> p s u")
-            if on_vector:
-                nc.vector.tensor_copy(woven[s].bitcast(I32).rearrange("p (s u) -> p s u", u=2), staged_i32(s, n))
-            else:
-                nc.scalar.copy(words, source)
-
-        def staged_i32(s, n):
-            return staged(s, n).bitcast(I32).rearrange("p u s -> p s u")
+            copy(woven[s].bitcast(word).rearrange("p (s u) -> p s u", u=2), staged(s, n).bitcast(word).rearrange("p u s -> p s u"))
 
         def quantise_x(s, n, takes_over=None):
             codes, scales = sbuf(f"x_codes{s}", n * SLAB, U32, takes_over), sbuf(f"x_scales{s}", n * SLAB, U8)
@@ -241,20 +235,19 @@ def tile_moe_two_glu_silu_kernel(
         quantise_x(1, 1)
         gather(1, 4, 2)
         quantise_x(2, 2)
+        weave(4, 2, nc.vector.tensor_copy, I32)
         gather(1, 6, 2)
-        weave(4, 2)
         quantise_x(4, 2)
-        weave(6, 2, True)
+        weave(6, 2, nc.gpsimd.tensor_copy, U32)
         pass_a(0)
         pass_a(1)
         pass_b(0)
-        pass_b(1)
         pass_a(2)
+        pass_b(1)
         pass_a(3)
         product(0)
         pass_b(2)
         product(1)
-        quantise_x(6, 2, "x_codes0")
         pass_a(4)
         pass_a(5)
         pass_b(3)
@@ -262,6 +255,7 @@ def tile_moe_two_glu_silu_kernel(
         turn(1)
         collect(0)
         product(2)
+        quantise_x(6, 2, "silu1")
         pass_b(4)
         product(3)
         quantise_h(0)

@@ -137,6 +137,20 @@ def tile_moe_two_glu_silu_kernel(
                 x_codes[s + i] = codes[:, i * SLAB : (i + 1) * SLAB]
                 x_scales[s + i] = scales[:, i * SLAB : (i + 1) * SLAB]
 
+        def warm_up():
+            codes, scales = sbuf("warm_codes", C, U32), sbuf("warm_scales", C, U8)
+            nc.vector.quantize_mx(out=codes.bitcast(FP8), scales=scales, in_=pairs[0][:, 0 : 4 * C])
+            for i in range(4):
+                nc.tensor.matmul_mx(
+                    out=bank[4 + i // 2][:, (i % 2) * C : (i % 2 + 1) * C],
+                    lhsT=weights["w1", 0][:, 0 : WORD * P].bitcast(FP4),
+                    lhsT_scale=scales[:, 0:P],
+                    rhs=codes.bitcast(FP8),
+                    rhs_scale=scales,
+                    start=True,
+                    stop=True,
+                )
+
         silu_a, sums_b, h_rows, h_turned, y_rows, window = {}, {}, {}, {}, {}, {}
 
         def by_pair(sums):
@@ -224,6 +238,7 @@ def tile_moe_two_glu_silu_kernel(
 
         for i in range(len(CHUNKS[0])):
             cast(0, i)
+        warm_up()
         for s in (0, 4):
             gather(0, s, 4)
         for i in range(len(CHUNKS[1])):

@@ -18,7 +18,7 @@ STAGE_BLOCK = (2, 3, 0, 1)
 
 A_BANK = (0, 1, 6, 7, 0, 1, 6, 7)
 B_BANK = (2, 3, 4, 2, 3, 4, 2, 3)
-TURN_BANK = (5, 0, 5, 6)
+TURN_BANK = (5, 5, 0, 0, 5, 5, 6, 2)
 Y_HALF = ((1, 4), (0, 7), (2, 5), (3, 1))
 
 F32 = mybir.dt.float32
@@ -151,7 +151,7 @@ def tile_moe_two_glu_silu_kernel(
                     stop=True,
                 )
 
-        silu_a, sums_b, h_rows, h_turned, y_rows, window = {}, {}, {}, {}, {}, {}
+        silu_a, h_rows, h_turned, y_rows, window = {}, {}, {}, {}, {}
 
         def by_pair(sums):
             return sums[:].rearrange("s (q u d) -> s u q d", u=2, d=2)
@@ -184,15 +184,18 @@ def tile_moe_two_glu_silu_kernel(
             nc.vector.tensor_tensor(in_pair_order(h_rows[s]), in_pair_order(silu_a[s]), by_pair(bank[B_BANK[s]]), MULT)
 
         def turn(s):
-            columns = bank[TURN_BANK[s // 2]][:].rearrange("p (b u s) -> p b u s", b=2, u=2)
+            columns = bank[TURN_BANK[s]][:].rearrange("p (b u s) -> p b u s", b=2, u=2)
             h_words = h_rows[s].bitcast(F32)
             for u in range(2):
                 nc.tensor.transpose(columns[:, s % 2, u, :], h_words[:, u * P : (u + 1) * P], ident)
 
-        def collect(e, takes_over=None, copy=nc.scalar.copy):
-            h_turned[e] = sbuf(f"turned{e}", C * 4, BF16, takes_over)
+        def collect(s, n, copy=nc.scalar.copy):
+            e = s // 2
+            if e not in h_turned:
+                h_turned[e] = sbuf(f"turned{e}", C * 4, BF16)
             words = h_turned[e].bitcast(F32).rearrange("p (b s u) -> p b s u", b=2, u=2)
-            copy(words, bank[TURN_BANK[e]][:].rearrange("p (b u s) -> p b s u", b=2, u=2))
+            turned = bank[TURN_BANK[s]][:].rearrange("p (b u s) -> p b s u", b=2, u=2)
+            copy(words[:, s % 2 : s % 2 + n], turned[:, s % 2 : s % 2 + n])
 
         h_codes = {}
 
@@ -268,7 +271,7 @@ def tile_moe_two_glu_silu_kernel(
         pass_b(3)
         turn(0)
         turn(1)
-        collect(0)
+        collect(0, 2)
         product(2)
         quantise_x(6, 2, "silu1")
         pass_b(4)
@@ -280,13 +283,13 @@ def tile_moe_two_glu_silu_kernel(
         pass_b(6)
         turn(2)
         turn(3)
-        collect(1)
+        collect(2, 2)
         product(4)
         pass_b(7)
         product(5)
         turn(4)
         turn(5)
-        collect(2)
+        collect(4, 2)
         down(0)
         product(6)
         product(7)
@@ -297,13 +300,14 @@ def tile_moe_two_glu_silu_kernel(
         turn(6)
         turn(7)
         down(1)
-        collect(3)
-        window[0] = sbuf("window0", T, F32, "h5")
-        window[1] = sbuf("window1", T, F32, "h7")
+        collect(6, 1)
+        collect(7, 1, nc.vector.tensor_copy)
+        window[0] = sbuf("window0", T, F32, "h_codes1")
+        window[1] = sbuf("window1", T, F32, "h6")
         scatter_half(0, 1)
         down(2)
-        gate_and_scatter(0, 0)
         gate_half(1, 1)
+        gate_and_scatter(0, 0)
         quantise_h(3)
         down(3)
         copy_half(1, 0)

@@ -143,7 +143,7 @@ def tile_moe_two_glu_silu_kernel(
             for i in range(4):
                 nc.tensor.matmul_mx(
                     out=bank[4 + i // 2][:, (i % 2) * C : (i % 2 + 1) * C],
-                    lhsT=weights["w1", 0][:, 0 : WORD * P].bitcast(FP4),
+                    lhsT=weights["w3", 0][:, 0 : WORD * P].bitcast(FP4),
                     lhsT_scale=scales[:, 0:P],
                     rhs=codes.bitcast(FP8),
                     rhs_scale=scales,

@@ -12,7 +12,10 @@ LIST = 16
 WORD = 2
 NEIGHBOURS = 4
 
-CHUNKS = (((0, 768, 480, 0), (768, 256, 160, 0)), ((0, 320, 0, 96), (320, 320, 0, 96), (640, 256, 0, 80), (896, 128, 0, 32)))
+CHUNKS = (
+    ((0, 512, 320, 0), (512, 256, 160, 0), (768, 256, 160, 0)),
+    ((0, 256, 0, 80), (256, 256, 0, 80), (512, 256, 0, 80), (768, 128, 0, 32), (896, 128, 0, 32)),
+)
 
 STAGE_BLOCK = (2, 3, 0, 1)
 
@@ -74,7 +77,7 @@ def tile_moe_two_glu_silu_kernel(
             for i, (t0, width, by_vector, by_gpsimd) in enumerate(CHUNKS[u]):
                 raw[u, i] = keep.tile([P, 2, width], F32, name=f"raw{u}{i}", align_bytes=256)[:]
                 nc.sync.dma_start(out=raw[u, i], in_=x_rows[:, 2 * u : 2 * u + 2, t0 : t0 + width])
-                if (u, i) == (0, 1):
+                if (u, i) == (0, len(CHUNKS[0]) - 1):
                     nc.sync.dma_start(offs_sb[:], offs)
         nc.scalar.activation(table_warm[:], table_warm[:], ACT.Silu)
         make_identity(nc, ident)
@@ -239,9 +242,10 @@ def tile_moe_two_glu_silu_kernel(
         def gate_and_scatter(e, m, lo=0, hi=C):
             nc.vector.tensor_tensor(places(e, m, lo, hi), y_rows[e, m, lo], gates(e)[:, lo:hi], MULT)
 
-        for i in range(len(CHUNKS[0])):
-            cast(0, i)
+        cast(0, 0)
         warm_up()
+        for i in range(1, len(CHUNKS[0])):
+            cast(0, i)
         for s in (0, 4):
             gather(0, s, 4)
         for i in range(len(CHUNKS[1])):

from contextlib import ExitStack

import concourse.mybir as mybir
from concourse.masks import make_identity

K, T, E, C, H, N = 512, 1024, 4, 256, 512, 256
FLOPS = 2 * E * C * (K * H + K * H + H * N)

P = 128
SLAB = 128
LIST = 16
WORD = 2
NEIGHBOURS = 4

CHUNKS = (
    ((0, 512, 320, 0), (512, 256, 160, 0), (768, 256, 160, 0)),
    ((0, 256, 0, 80), (256, 256, 0, 80), (512, 256, 0, 80), (768, 128, 0, 32), (896, 128, 0, 32)),
)

STAGE_BLOCK = (2, 3, 0, 1)

A_BANK = (0, 1, 6, 7, 0, 1, 6, 7)
B_BANK = (2, 3, 4, 2, 3, 4, 2, 3)
TURN_BANK = (5, 5, 0, 0, 5, 5, 6, 2)
Y_HALF = ((1, 4), (0, 7), (2, 5), (3, 1))

F32 = mybir.dt.float32
BF16 = mybir.dt.bfloat16
I32 = mybir.dt.int32
U32 = mybir.dt.uint32
U16 = mybir.dt.uint16
U8 = mybir.dt.uint8
FP8 = mybir.dt.float8_e4m3fn_x4
FP4 = mybir.dt.float4_e2m1fn_x4
ACT = mybir.ActivationFunctionType
MULT = mybir.AluOpType.mult


def tile_moe_two_glu_silu_kernel(
    tc, xT, w1_words, w1_scales, w3_words, w3_scales, w2_words, w2_scales, gate, offs, dst, out
):
    nc = tc.nc
    with ExitStack() as ctx:
        keep = ctx.enter_context(tc.tile_pool(name="keep", bufs=1))
        psum = ctx.enter_context(tc.psum_pool(name="psum", bufs=1))

        def sbuf(name, columns, dtype, takes_over=None):
            return keep.tile([P, columns], dtype, name=name, align_bytes=256, tag=takes_over or name)[:]

        offs_sb = keep.tile([P, E * C // LIST], U16, name="offs_sb")
        dst_sb = keep.tile([P, E * C // LIST], U16, name="dst_sb")
        w1_plane = sbuf("w1_plane", E * H, U8)
        w3_plane = sbuf("w3_plane", E * H, U8)
        w2_plane = sbuf("w2_plane", E * N, U8)
        pairs = [sbuf(f"pairs{u}", 2 * T, BF16) for u in range(2)]
        stage = sbuf("stage", (E + 3) * C, U32)
        ident = sbuf("ident", P, F32)
        half_slots = E * C // 2
        gate_sb = [sbuf(f"gate{i}", half_slots, F32) for i in range(2)]
        bank = [psum.tile([P, 4 * SLAB], F32, name=f"bank{i}") for i in range(8)]

        table_warm = keep.tile([P, 1], F32, name="table_warm")
        nc.vector.memset(table_warm[:], 0.0)
        for plane in (w1_plane, w3_plane, w2_plane):
            nc.vector.memset(plane.bitcast(I32), 0)

        def load_scales(plane, src, quadrants=(0, 2, 1, 3)):
            for q in quadrants:
                nc.sync.dma_start(
                    out=plane[32 * q : 32 * q + 4, :].rearrange("r (e i) -> r e i", e=E).bitcast(I32),
                    in_=src[:, 0, 4 * q : 4 * q + 4, :].rearrange("e r i -> r e i").bitcast(I32),
                )

        x_rows = xT.rearrange("(p j) t -> p j t", j=4)
        raw = {}
        for u in range(2):
            for i, (t0, width, by_vector, by_gpsimd) in enumerate(CHUNKS[u]):
                raw[u, i] = keep.tile([P, 2, width], F32, name=f"raw{u}{i}", align_bytes=256)[:]
                nc.sync.dma_start(out=raw[u, i], in_=x_rows[:, 2 * u : 2 * u + 2, t0 : t0 + width])
                if (u, i) == (0, len(CHUNKS[0]) - 1):
                    nc.sync.dma_start(offs_sb[:], offs)
        nc.scalar.activation(table_warm[:], table_warm[:], ACT.Silu)
        make_identity(nc, ident)

        weights = {}

        def load_words(key, src, e0, n):
            rows = sbuf(f"{key}_words{e0}", n * src.shape[3], U8).rearrange("p (e b) -> p e b", e=n)
            nc.sync.dma_start(out=rows.bitcast(I32), in_=src[e0 : e0 + n, 0].rearrange("e p b -> p e b").bitcast(I32))
            for i in range(n):
                weights[key, e0 + i] = rows[:, i, :]

        load_words("w3", w3_words, 0, 1)
        load_scales(w3_plane, w3_scales, (0, 2, 1))
        load_words("w1", w1_words, 0, 2)
        load_scales(w1_plane, w1_scales, (2, 0, 3, 1))
        load_scales(w3_plane, w3_scales, (3,))
        load_words("w3", w3_words, 1, 1)
        load_words("w1", w1_words, 2, 2)
        load_words("w3", w3_words, 2, 2)
        load_scales(w2_plane, w2_scales)
        load_words("w2", w2_words, 0, E)
        nc.sync.dma_start(out=gate_sb[0], in_=gate[0:P, 0:half_slots])
        nc.sync.dma_start(dst_sb[:], dst)
        nc.sync.dma_start(out=gate_sb[1], in_=gate[0:P, half_slots:])

        def cast(u, i):
            t0, width, by_vector, by_gpsimd = CHUNKS[u][i]
            for lo, hi, copy in ((0, by_vector, nc.vector.tensor_copy), (by_vector, width - by_gpsimd, nc.scalar.copy)):
                if lo < hi:
                    values = pairs[u][:, 2 * (t0 + lo) : 2 * (t0 + hi)].rearrange("p (c t j) -> p c j t", t=NEIGHBOURS, j=2)
                    copy(values, raw[u, i][:, :, lo:hi].rearrange("p j (c t) -> p c j t", t=NEIGHBOURS))
            if by_gpsimd:
                values = pairs[u][:, 2 * (t0 + width - by_gpsimd) : 2 * (t0 + width)].rearrange("p (t j) -> p t j", j=2)
                nc.gpsimd.tensor_copy(values, raw[u, i][:, :, width - by_gpsimd : width].rearrange("p j t -> p t j"))

        def staged(s, n):
            e, lo = divmod(s * SLAB, C)
            both = stage.rearrange("p (b s) -> p b s", s=C)[:, STAGE_BLOCK[e] : STAGE_BLOCK[e] + 3 : 2, :]
            return both[:, :, lo : lo + n * SLAB]

        def gather(u, s, n):
            offsets = offs_sb[:, s * SLAB // LIST : (s + n) * SLAB // LIST]
            first = (STAGE_BLOCK[s * SLAB // C] + 2 * u) * C + s * SLAB % C
            nc.vector.tensor_copy(stage[:, first : first + n * SLAB], pairs[u].bitcast(U32).indirect(offsets))

        woven, x_codes, x_scales = {}, {}, {}

        def weave(s, n, copy=nc.scalar.copy, word=U32, takes_over=None):
            if s >= 4:
                woven[s] = stage[:, (E + 1) * C : (E + 3) * C].bitcast(BF16)
            else:
                woven[s] = sbuf(f"woven{s}", 4 * n * SLAB, BF16, takes_over)
            copy(woven[s].bitcast(word).rearrange("p (s u) -> p s u", u=2), staged(s, n).bitcast(word).rearrange("p u s -> p s u"))

        def quantise_x(s, n, takes_over=None):
            codes, scales = sbuf(f"x_codes{s}", n * SLAB, U32, takes_over), sbuf(f"x_scales{s}", n * SLAB, U8)
            nc.vector.quantize_mx(out=codes.bitcast(FP8), scales=scales, in_=woven[s])
            for i in range(n):
                x_codes[s + i] = codes[:, i * SLAB : (i + 1) * SLAB]
                x_scales[s + i] = scales[:, i * SLAB : (i + 1) * SLAB]

        def warm_up():
            codes, scales = sbuf("warm_codes", C, U32), sbuf("warm_scales", C, U8)
            nc.vector.quantize_mx(out=codes.bitcast(FP8), scales=scales, in_=pairs[0][:, 0 : 4 * C])
            for i in range(4):
                nc.tensor.matmul_mx(
                    out=bank[4 + i // 2][:, (i % 2) * C : (i % 2 + 1) * C],
                    lhsT=weights["w3", 0][:, 0 : WORD * P].bitcast(FP4),
                    lhsT_scale=scales[:, 0:P],
                    rhs=codes.bitcast(FP8),
                    rhs_scale=scales,
                    start=True,
                    stop=True,
                )

        silu_a, h_rows, h_turned, y_rows, window = {}, {}, {}, {}, {}

        def by_pair(sums):
            return sums[:].rearrange("s (q u d) -> s u q d", u=2, d=2)

        def in_pair_order(tile):
            return tile.rearrange("s (u q d) -> s u q d", u=2, d=2)

        def first_layer(s, sums, key, plane):
            e = s * SLAB // C
            nc.tensor.matmul_mx(
                out=sums[:],
                lhsT=x_codes[s].bitcast(FP8),
                lhsT_scale=x_scales[s],
                rhs=weights[key, e].bitcast(FP4),
                rhs_scale=plane[:, e * H : (e + 1) * H],
                start=True,
                stop=True,
            )

        def pass_a(s):
            first_layer(s, bank[A_BANK[s]], "w1", w1_plane)
            silu_a[s] = sbuf(f"silu{s}", H, F32)
            nc.scalar.activation(in_pair_order(silu_a[s]), by_pair(bank[A_BANK[s]]), ACT.Silu)

        def pass_b(s):
            first_layer(s, bank[B_BANK[s]], "w3", w3_plane)

        def product(s, takes_over=None):
            h_rows[s] = sbuf(f"h{s}", H, BF16, takes_over)
            nc.vector.tensor_tensor(in_pair_order(h_rows[s]), in_pair_order(silu_a[s]), by_pair(bank[B_BANK[s]]), MULT)

        def turn(s):
            columns = bank[TURN_BANK[s]][:].rearrange("p (b u s) -> p b u s", b=2, u=2)
            h_words = h_rows[s].bitcast(F32)
            for u in range(2):
                nc.tensor.transpose(columns[:, s % 2, u, :], h_words[:, u * P : (u + 1) * P], ident)

        def collect(s, n, copy=nc.scalar.copy):
            e = s // 2
            if e not in h_turned:
                h_turned[e] = sbuf(f"turned{e}", C * 4, BF16)
            words = h_turned[e].bitcast(F32).rearrange("p (b s u) -> p b s u", b=2, u=2)
            turned = bank[TURN_BANK[s]][:].rearrange("p (b u s) -> p b s u", b=2, u=2)
            copy(words[:, s % 2 : s % 2 + n], turned[:, s % 2 : s % 2 + n])

        h_codes = {}

        def quantise_h(e):
            h_codes[e] = sbuf(f"h_codes{e}", C, U32), sbuf(f"h_scales{e}", C, U8)
            nc.vector.quantize_mx(out=h_codes[e][0].bitcast(FP8), scales=h_codes[e][1], in_=h_turned[e])

        def down(e):
            codes, scales = h_codes[e]
            for m in (1, 0):
                nc.tensor.matmul_mx(
                    out=bank[Y_HALF[e][m]][:, m * C : (m + 1) * C],
                    lhsT=weights["w2", e][:, WORD * m * P : WORD * (m + 1) * P].bitcast(FP4),
                    lhsT_scale=w2_plane[:, e * N + m * P : e * N + (m + 1) * P],
                    rhs=codes.bitcast(FP8),
                    rhs_scale=scales,
                    start=True,
                    stop=True,
                )

        def gates(e):
            return gate_sb[e * C // half_slots][:, e * C % half_slots : e * C % half_slots + C]

        def sums(e, m, lo, hi):
            return bank[Y_HALF[e][m]][:, m * C + lo : m * C + hi]

        def gate_half(e, m, takes_over=None, lo=0, hi=C):
            y_rows[e, m, lo] = sbuf(f"y{e}{m}_{lo}", hi - lo, F32, takes_over)
            nc.vector.tensor_tensor(y_rows[e, m, lo], sums(e, m, lo, hi), gates(e)[:, lo:hi], MULT)

        def copy_half(e, m, takes_over=None, lo=0, hi=C):
            y_rows[e, m, lo] = sbuf(f"y{e}{m}_{lo}", hi - lo, F32, takes_over)
            nc.scalar.copy(y_rows[e, m, lo], sums(e, m, lo, hi))

        def places(e, m, lo, hi):
            return window[m].indirect(dst_sb[:, (e * C + lo) // LIST : (e * C + hi) // LIST])

        def scatter_half(e, m, lo=0, hi=C):
            nc.scalar.activation(places(e, m, lo, hi), y_rows[e, m, lo], ACT.Copy)

        def gate_and_scatter(e, m, lo=0, hi=C):
            nc.vector.tensor_tensor(places(e, m, lo, hi), y_rows[e, m, lo], gates(e)[:, lo:hi], MULT)

        cast(0, 0)
        warm_up()
        for i in range(1, len(CHUNKS[0])):
            cast(0, i)
        for s in (0, 4):
            gather(0, s, 4)
        for i in range(len(CHUNKS[1])):
            cast(1, i)
        for s, n in ((0, 1), (1, 1), (2, 2)):
            gather(1, s, n)
            weave(s, n)
        quantise_x(0, 1)
        quantise_x(1, 1)
        gather(1, 4, 2)
        quantise_x(2, 2)
        weave(4, 2, nc.vector.tensor_copy, I32)
        gather(1, 6, 2)
        quantise_x(4, 2)
        weave(6, 2, nc.gpsimd.tensor_copy, U32)
        pass_a(0)
        pass_a(1)
        pass_b(0)
        pass_a(2)
        pass_b(1)
        pass_a(3)
        product(0)
        pass_b(2)
        product(1)
        pass_a(4)
        pass_a(5)
        pass_b(3)
        turn(0)
        turn(1)
        collect(0, 2)
        product(2)
        quantise_x(6, 2, "silu1")
        pass_b(4)
        product(3)
        quantise_h(0)
        pass_a(6)
        pass_a(7)
        pass_b(5)
        pass_b(6)
        turn(2)
        turn(3)
        collect(2, 2)
        product(4)
        pass_b(7)
        product(5)
        turn(4)
        turn(5)
        collect(4, 2)
        down(0)
        product(6)
        product(7)
        quantise_h(1)
        copy_half(0, 0)
        gate_half(0, 1)
        quantise_h(2)
        turn(6)
        turn(7)
        down(1)
        collect(6, 1)
        collect(7, 1, nc.vector.tensor_copy)
        window[0] = sbuf("window0", T, F32, "h_codes1")
        window[1] = sbuf("window1", T, F32, "h6")
        scatter_half(0, 1)
        down(2)
        gate_half(1, 1)
        gate_and_scatter(0, 0)
        quantise_h(3)
        down(3)
        copy_half(1, 0)
        scatter_half(1, 1)
        gate_half(2, 1)
        gate_and_scatter(1, 0)
        copy_half(2, 0, "turned3")
        scatter_half(2, 1)
        gate_half(3, 1)
        gate_and_scatter(2, 0)
        copy_half(3, 0)
        scatter_half(3, 1)
        gate_and_scatter(3, 0)
        for m in (1, 0):
            nc.sync.dma_start(out=out[m * P : (m + 1) * P, :], in_=window[m])
